import numpy as np
import ml_dtypes


def mxq(x, axis, fmt="e4m3"):
    dtype, down = {"e4m3": (ml_dtypes.float8_e4m3fn, 7), "e5m2": (ml_dtypes.float8_e5m2, 14)}[fmt]
    v = np.moveaxis(np.asarray(x, np.float32).astype(ml_dtypes.bfloat16).astype(np.float64), axis, -1)
    blocks = v.reshape(v.shape[:-1] + (-1, 32))
    amax = np.abs(blocks).max(-1, keepdims=True)
    byte = np.maximum(np.where(amax > 0, np.frexp(amax)[1] - 1 + 127, 0) - down, 1)
    scale = np.exp2(byte - 127.0)
    codes = (blocks / scale).astype(np.float32).astype(dtype).astype(np.float64)
    return np.moveaxis((codes * scale).reshape(v.shape), -1, axis)


WIDE = False


def mx_kscale(k):
    if not WIDE:
        return np.ones(k)
    levels = np.array([10, -10, 5, -5, 0])
    if k % 512:
        return np.exp2(np.random.permutation(np.resize(levels, k // 32))).repeat(32)
    a = np.empty((k // 512, 16))
    for p in range(k // 512):
        a[p, :8] = np.random.permutation(np.resize(levels, 8))
        for g in range(8):
            far = levels[np.abs(levels - a[p, g]) >= 10]
            a[p, g + 8] = far[np.random.randint(len(far))]
    return np.exp2(a.ravel()).repeat(32)


def f64(x):
    return np.asarray(x).astype(np.float64)


def striped(idx):
    return np.tile(idx.reshape(-1, 16).T, (8, 1)).astype(np.uint16)


def unstriped(offs):
    return offs[:16].T.reshape(-1).astype(np.int64)


def pack_weight(w):
    k, n = w.shape
    w = f64(np.asarray(w, np.float32).astype(ml_dtypes.bfloat16)).reshape(k // 32, 32, n)
    amax = np.abs(w).max(1)
    byte = np.clip(np.where(amax > 0, np.frexp(amax)[1] - 1 + 127 - 7, 1), 1, 254)
    scaled = (w * np.exp2(127.0 - byte)[:, None, :]).reshape(k, n).astype(np.float32)
    words = np.ascontiguousarray(scaled.reshape(k // 512, 128, 4, n).transpose(0, 1, 3, 2)).astype(ml_dtypes.float8_e4m3fn).view(np.uint8)
    return words, np.ascontiguousarray(byte.astype(np.uint8).reshape(k // 512, 16, n))


def unpack_weight(words, scales):
    g, p, n, _ = words.shape
    vals = np.ascontiguousarray(words).view(ml_dtypes.float8_e4m3fn).astype(np.float64) * np.repeat(np.exp2(scales.astype(np.float64) - 127.0), 8, axis=1)[..., None]
    return vals.transpose(0, 1, 3, 2).reshape(g * 512, n)

def planes(y):
    n, m = y.shape
    v = y.astype(np.float32).astype(ml_dtypes.bfloat16).astype(np.float64).reshape(n // 32, 32, m)
    top = np.abs(v).max(1)
    byte = np.clip(np.where(top > 0, np.frexp(top)[1] - 1 + 127 - 7, 1), 1, 254)
    codes = (v * np.exp2(127.0 - byte)[:, None, :]).reshape(n, m).astype(np.float32).astype(ml_dtypes.float8_e4m3fn).view(np.uint8)
    words = codes.reshape(n // 512, 128, 4, m).transpose(0, 1, 3, 2)
    return np.ascontiguousarray(words), np.ascontiguousarray(byte.astype(np.uint8).reshape(n // 512, 16, m))


K, T, N, U = 512, 512, 512, 1024
P = 2 ** 7


def setup_inputs():
    n = np.random.standard_normal
    s = mx_kscale(K)[:, None]
    packed_xT = pack_weight(n((K, T)) * s)
    return {
        "x_words": packed_xT[0],
        "x_scales": packed_xT[1],
        "gate": np.tile(np.random.uniform(0.5, 1.5, T), (P, 1)).astype(np.float32),
        "w1": (n((K, N)) / np.sqrt(K) / s).astype(np.float32),
        "dst": striped(np.random.permutation(U)[:T]),
    }


def reference(x_words, x_scales, gate, w1, dst):
    xq = unpack_weight(x_words, x_scales)
    y = mxq(f64(w1), 0, "e4m3").T @ xq
    out = np.zeros((N, U))
    out[:, unstriped(dst)] = y * f64(gate)[:1]
    return (out,) + planes(out)

@@ -1,0 +1,126 @@
+from contextlib import ExitStack
+
+import concourse.mybir as mybir
+
+K, T, N, U = 512, 512, 512, 1024
+FLOPS = 2 * K * T * N
+
+F32 = mybir.dt.float32
+BF16 = mybir.dt.bfloat16
+I32 = mybir.dt.int32
+U32 = mybir.dt.uint32
+U16 = mybir.dt.uint16
+U8 = mybir.dt.uint8
+FP8X4 = mybir.dt.float8_e4m3fn_x4
+MULT = mybir.AluOpType.mult
+
+P = 128
+PACK = 4
+W_CHUNKS = ((0, 256), (256, 384), (384, 512))
+HEAD = 128
+
+
+def tile_picked_wroute2_linnone_lo_kernel(tc, x_words, x_scales, gate, w1, dst, out_0, out_1, out_2):
+    nc = tc.nc
+    with ExitStack() as ctx:
+        keep = ctx.enter_context(tc.tile_pool(name="keep", bufs=1))
+        psum = ctx.enter_context(tc.psum_pool(name="psum", bufs=1))
+
+        offsets = keep.tile([P, T // 16], U16, name="offsets")
+        x_codes = keep.tile([P, T], U32, name="x_codes", align_bytes=64)
+        x_plane = keep.tile([P, T], U8, name="x_plane", align_bytes=64)
+        gate_sb = keep.tile([P, T], F32, name="gate_sb")
+        w_grouped = keep.tile([P, N * PACK], BF16, name="w_grouped", align_bytes=64)
+        w_codes = keep.tile([P, N], U32, name="w_codes", align_bytes=64)
+        w_plane = keep.tile([P, N], U8, name="w_plane", align_bytes=64)
+        y_grouped = keep.tile([P, U * PACK], BF16, name="y_grouped", align_bytes=64)
+        y_codes = keep.tile([P, U], U32, name="y_codes", align_bytes=64)
+        y_plane = keep.tile([P, U], U8, name="y_plane", align_bytes=64)
+        windows = [keep.tile([P, U], F32, name="window%d" % t) for t in range(PACK)]
+        staged = [keep.tile([P, T], F32, name="staged%d" % t) for t in range(PACK)]
+        w_raw = [keep.tile([P, PACK, b - a], F32, name="w_raw%d" % a) for a, b in W_CHUNKS]
+
+        first, second, third, last = 2, 0, 1, 3
+
+        nc.vector.memset(x_plane[:].bitcast(I32), 0)
+        w_rows = w1.rearrange("(p j) c -> p j c", j=PACK)
+        for raw, (a, b) in zip(w_raw, W_CHUNKS):
+            nc.sync.dma_start(out=raw[:], in_=w_rows[:, :, a:b])
+        for q in range(4):
+            nc.sync.dma_start(out=x_plane[32 * q : 32 * q + 4, :].bitcast(I32), in_=x_scales[0][4 * q : 4 * q + 4, :].bitcast(I32))
+        nc.sync.dma_start(offsets[:], dst)
+        nc.sync.dma_start(out=x_codes[:].bitcast(I32), in_=x_words[0].rearrange("p n t -> p (n t)").bitcast(I32))
+        nc.sync.dma_start(out=gate_sb[:], in_=gate)
+
+        for t in (first, second, third, last):
+            nc.vector.memset(windows[t][:], 0.0)
+
+        w_view = w_grouped[:].rearrange("p (t m j) -> p m t j", t=PACK, j=PACK)
+        for raw, (a, b) in zip(w_raw, W_CHUNKS):
+            nc.vector.tensor_copy(out=w_view[:, a // PACK : b // PACK], in_=raw[:].rearrange("p j (m t) -> p m t j", t=PACK))
+
+        def quantize_w(t0, t1):
+            nc.vector.quantize_mx(
+                out=w_codes[:, P * t0 : P * t1].bitcast(FP8X4),
+                scales=w_plane[:, P * t0 : P * t1],
+                in_=w_grouped[:, PACK * P * t0 : PACK * P * t1],
+            )
+
+        def project(t, pieces, name):
+            lo, hi = pieces[0][0], pieces[-1][1]
+            acc = psum.tile([P, hi - lo], F32, name=name)
+            for a, b in pieces:
+                nc.tensor.matmul_mx(
+                    out=acc[:, a - lo : b - lo],
+                    lhsT=w_codes[:, P * t : P * (t + 1)].bitcast(FP8X4),
+                    lhsT_scale=w_plane[:, P * t : P * (t + 1)],
+                    rhs=x_codes[:, a:b].bitcast(FP8X4),
+                    rhs_scale=x_plane[:, a:b],
+                    start=True,
+                    stop=True,
+                )
+            nc.scalar.copy(out=staged[t][:, lo:hi], in_=acc[:])
+
+        def scatter(t, a, b):
+            nc.vector.tensor_tensor(
+                windows[t][:].indirect(offsets[:, a // 16 : b // 16]), staged[t][:, a:b], gate_sb[:, a:b], MULT
+            )
+
+        quantize_w(first, first + 1)
+        project(first, [(0, HEAD)], "acc_head")
+        project(first, [(HEAD, 2 * HEAD), (2 * HEAD, T)], "acc_first")
+        quantize_w(second, third + 1)
+        quantize_w(last, last + 1)
+        for t in (second, third, last):
+            project(t, [(0, T)], "acc%d" % t)
+
+        out_rows = out_0.rearrange("(p t) c -> p t c", t=PACK)
+        y_view = y_grouped[:].rearrange("p (c t) -> p c t", t=PACK)
+
+        scatter(first, 0, HEAD)
+        scatter(first, HEAD, T)
+        nc.sync.dma_start(out=out_rows[:, first, :], in_=windows[first][:])
+        nc.scalar.copy(out=y_view[:, :, first : first + 2], in_=windows[first][:].unsqueeze(2).to_broadcast([P, U, 2]))
+        scatter(second, 0, T)
+        nc.sync.dma_start(out=out_rows[:, second, :], in_=windows[second][:])
+        nc.scalar.copy(out=y_view[:, :, second], in_=windows[second][:])
+        scatter(third, 0, T)
+        nc.sync.dma_start(out=out_rows[:, third, :], in_=windows[third][:])
+        for a, b in ((0, 512), (512, 768), (768, 1024)):
+            nc.scalar.copy(out=y_view[:, a:b, third], in_=windows[third][:, a:b])
+        scatter(last, 0, T)
+        nc.sync.dma_start(out=out_rows[:, last, :], in_=windows[last][:])
+        nc.vector.tensor_copy(out=y_view[:, 0:512, last], in_=windows[last][:, 0:512])
+        nc.scalar.copy(out=y_view[:, 512:768, last], in_=windows[last][:, 512:768])
+        nc.vector.tensor_copy(out=y_view[:, 768:896, last], in_=windows[last][:, 768:896])
+        nc.scalar.copy(out=y_view[:, 896:1024, last], in_=windows[last][:, 896:1024])
+
+        words_out = out_1[0].rearrange("p n t -> p (n t)").bitcast(I32)
+        for a, b in ((0, 512), (512, 768), (768, 1024)):
+            nc.vector.quantize_mx(
+                out=y_codes[:, a:b].bitcast(FP8X4), scales=y_plane[:, a:b], in_=y_grouped[:, PACK * a : PACK * b]
+            )
+            nc.sync.dma_start(out=words_out[:, a:b], in_=y_codes[:, a:b].bitcast(I32))
+        for q in range(4):
+            queue = nc.sync if q % 2 else nc.scalar
+            queue.dma_start(out=out_2[0][4 * q : 4 * q + 4, :].bitcast(I32), in_=y_plane[32 * q : 32 * q + 4, :].bitcast(I32))

@@ -18,6 +18,7 @@ P = 128
 PACK = 4
 W_CHUNKS = ((0, 256), (256, 384), (384, 512))
 HEAD = 128
+X_ROW = 4
 
 
 def tile_picked_wroute2_linnone_lo_kernel(tc, x_words, x_scales, gate, w1, dst, out_0, out_1, out_2):
@@ -28,11 +29,10 @@ def tile_picked_wroute2_linnone_lo_kernel(tc, x_words, x_scales, gate, w1, dst, 
 
         offsets = keep.tile([P, T // 16], U16, name="offsets")
         x_codes = keep.tile([P, T], U32, name="x_codes", align_bytes=64)
-        x_plane = keep.tile([P, T], U8, name="x_plane", align_bytes=64)
+        scales = keep.tile([P, T], U8, name="scales", align_bytes=64)
         gate_sb = keep.tile([P, T], F32, name="gate_sb")
         w_grouped = keep.tile([P, N * PACK], BF16, name="w_grouped", align_bytes=64)
         w_codes = keep.tile([P, N], U32, name="w_codes", align_bytes=64)
-        w_plane = keep.tile([P, N], U8, name="w_plane", align_bytes=64)
         y_grouped = keep.tile([P, U * PACK], BF16, name="y_grouped", align_bytes=64)
         y_codes = keep.tile([P, U], U32, name="y_codes", align_bytes=64)
         y_plane = keep.tile([P, U], U8, name="y_plane", align_bytes=64)
@@ -40,29 +40,35 @@ def tile_picked_wroute2_linnone_lo_kernel(tc, x_words, x_scales, gate, w1, dst, 
         staged = [keep.tile([P, T], F32, name="staged%d" % t) for t in range(PACK)]
         w_raw = [keep.tile([P, PACK, b - a], F32, name="w_raw%d" % a) for a, b in W_CHUNKS]
 
-        first, second, third, last = 2, 0, 1, 3
+        first, second, third, last = 0, 2, 3, 1
 
-        nc.vector.memset(x_plane[:].bitcast(I32), 0)
+        nc.sync.dma_start(offsets[:], dst)
         w_rows = w1.rearrange("(p j) c -> p j c", j=PACK)
         for raw, (a, b) in zip(w_raw, W_CHUNKS):
             nc.sync.dma_start(out=raw[:], in_=w_rows[:, :, a:b])
         for q in range(4):
-            nc.sync.dma_start(out=x_plane[32 * q : 32 * q + 4, :].bitcast(I32), in_=x_scales[0][4 * q : 4 * q + 4, :].bitcast(I32))
-        nc.sync.dma_start(offsets[:], dst)
+            rows = slice(32 * q + X_ROW, 32 * q + X_ROW + 4)
+            nc.sync.dma_start(out=scales[rows, :].bitcast(I32), in_=x_scales[0][4 * q : 4 * q + 4, :].bitcast(I32))
         nc.sync.dma_start(out=x_codes[:].bitcast(I32), in_=x_words[0].rearrange("p n t -> p (n t)").bitcast(I32))
         nc.sync.dma_start(out=gate_sb[:], in_=gate)
 
-        for t in (first, second, third, last):
-            nc.vector.memset(windows[t][:], 0.0)
+        for t in (first, second, third, last)[:3]:
+            nc.vector.memset(windows[t][:].bitcast(I32), 0)
+        for t in (first, second, third, last)[3:]:
+            nc.gpsimd.memset(windows[t][:].bitcast(I32), 0)
 
         w_view = w_grouped[:].rearrange("p (t m j) -> p m t j", t=PACK, j=PACK)
-        for raw, (a, b) in zip(w_raw, W_CHUNKS):
-            nc.vector.tensor_copy(out=w_view[:, a // PACK : b // PACK], in_=raw[:].rearrange("p j (m t) -> p m t j", t=PACK))
+        raw_views = [raw[:].rearrange("p j (m t) -> p m t j", t=PACK) for raw in w_raw]
+        nc.scalar.copy(out=w_view[:, 0:32], in_=raw_views[0][:, 0:32])
+        nc.vector.tensor_copy(out=w_view[:, 32:64], in_=raw_views[0][:, 32:64])
+        nc.vector.tensor_copy(out=w_view[:, 64:96], in_=raw_views[1])
+        nc.scalar.copy(out=w_view[:, 96:128, 0], in_=raw_views[2][:, :, 0])
+        nc.vector.tensor_copy(out=w_view[:, 96:128, 1:4], in_=raw_views[2][:, :, 1:4])
 
         def quantize_w(t0, t1):
             nc.vector.quantize_mx(
                 out=w_codes[:, P * t0 : P * t1].bitcast(FP8X4),
-                scales=w_plane[:, P * t0 : P * t1],
+                scales=scales[:, P * t0 : P * t1],
                 in_=w_grouped[:, PACK * P * t0 : PACK * P * t1],
             )
 
@@ -73,9 +79,9 @@ def tile_picked_wroute2_linnone_lo_kernel(tc, x_words, x_scales, gate, w1, dst, 
                 nc.tensor.matmul_mx(
                     out=acc[:, a - lo : b - lo],
                     lhsT=w_codes[:, P * t : P * (t + 1)].bitcast(FP8X4),
-                    lhsT_scale=w_plane[:, P * t : P * (t + 1)],
+                    lhsT_scale=scales[:, P * t : P * (t + 1)],
                     rhs=x_codes[:, a:b].bitcast(FP8X4),
-                    rhs_scale=x_plane[:, a:b],
+                    rhs_scale=scales[X_ROW:P, a:b],
                     start=True,
                     stop=True,
                 )
@@ -88,9 +94,9 @@ def tile_picked_wroute2_linnone_lo_kernel(tc, x_words, x_scales, gate, w1, dst, 
 
         quantize_w(first, first + 1)
         project(first, [(0, HEAD)], "acc_head")
-        project(first, [(HEAD, 2 * HEAD), (2 * HEAD, T)], "acc_first")
-        quantize_w(second, third + 1)
         quantize_w(last, last + 1)
+        quantize_w(second, third + 1)
+        project(first, [(HEAD, 2 * HEAD), (2 * HEAD, T)], "acc_first")
         for t in (second, third, last):
             project(t, [(0, T)], "acc%d" % t)
 
@@ -106,21 +112,23 @@ def tile_picked_wroute2_linnone_lo_kernel(tc, x_words, x_scales, gate, w1, dst, 
         nc.scalar.copy(out=y_view[:, :, second], in_=windows[second][:])
         scatter(third, 0, T)
         nc.sync.dma_start(out=out_rows[:, third, :], in_=windows[third][:])
-        for a, b in ((0, 512), (512, 768), (768, 1024)):
+        for a, b in [[0,256],[256,512],[512,768],[768,1024]]:
             nc.scalar.copy(out=y_view[:, a:b, third], in_=windows[third][:, a:b])
         scatter(last, 0, T)
         nc.sync.dma_start(out=out_rows[:, last, :], in_=windows[last][:])
-        nc.vector.tensor_copy(out=y_view[:, 0:512, last], in_=windows[last][:, 0:512])
+        nc.vector.tensor_copy(out=y_view[:, 0:256, last], in_=windows[last][:, 0:256])
         nc.scalar.copy(out=y_view[:, 512:768, last], in_=windows[last][:, 512:768])
-        nc.vector.tensor_copy(out=y_view[:, 768:896, last], in_=windows[last][:, 768:896])
-        nc.scalar.copy(out=y_view[:, 896:1024, last], in_=windows[last][:, 896:1024])
+        nc.vector.tensor_copy(out=y_view[:, 256:512, last], in_=windows[last][:, 256:512])
+        nc.scalar.copy(out=y_view[:, 768:1024, last], in_=windows[last][:, 768:1024])
 
         words_out = out_1[0].rearrange("p n t -> p (n t)").bitcast(I32)
-        for a, b in ((0, 512), (512, 768), (768, 1024)):
+        for a, b in [[0,256],[256,512],[512,768],[768,1024]]:
             nc.vector.quantize_mx(
                 out=y_codes[:, a:b].bitcast(FP8X4), scales=y_plane[:, a:b], in_=y_grouped[:, PACK * a : PACK * b]
             )
-            nc.sync.dma_start(out=words_out[:, a:b], in_=y_codes[:, a:b].bitcast(I32))
+            if b in {512: 0, 768: 512, 1024: 768}:
+                a = {512: 0, 768: 512, 1024: 768}[b]
+                nc.sync.dma_start(out=words_out[:, a:b], in_=y_codes[:, a:b].bitcast(I32))
         for q in range(4):
             queue = nc.sync if q % 2 else nc.scalar
             queue.dma_start(out=out_2[0][4 * q : 4 * q + 4, :].bitcast(I32), in_=y_plane[32 * q : 32 * q + 4, :].bitcast(I32))

@@ -16,7 +16,6 @@ MULT = mybir.AluOpType.mult
 
 P = 128
 PACK = 4
-W_CHUNKS = ((0, 256), (256, 384), (384, 512))
 HEAD = 128
 X_ROW = 4
 
@@ -38,17 +37,17 @@ def tile_picked_wroute2_linnone_lo_kernel(tc, x_words, x_scales, gate, w1, dst, 
         y_plane = keep.tile([P, U], U8, name="y_plane", align_bytes=64)
         windows = [keep.tile([P, U], F32, name="window%d" % t) for t in range(PACK)]
         staged = [keep.tile([P, T], F32, name="staged%d" % t) for t in range(PACK)]
-        w_raw = [keep.tile([P, PACK, b - a], F32, name="w_raw%d" % a) for a, b in W_CHUNKS]
+        w_raw = [keep.tile([P, 2, N], F32, name="w_raw%d" % u) for u in range(2)]
 
         first, second, third, last = 0, 2, 3, 1
 
-        nc.sync.dma_start(offsets[:], dst)
         w_rows = w1.rearrange("(p j) c -> p j c", j=PACK)
-        for raw, (a, b) in zip(w_raw, W_CHUNKS):
-            nc.sync.dma_start(out=raw[:], in_=w_rows[:, :, a:b])
+        for u in range(2):
+            nc.sync.dma_start(out=w_raw[u][:], in_=w_rows[:, 2 * u : 2 * u + 2, :])
         for q in range(4):
             rows = slice(32 * q + X_ROW, 32 * q + X_ROW + 4)
             nc.sync.dma_start(out=scales[rows, :].bitcast(I32), in_=x_scales[0][4 * q : 4 * q + 4, :].bitcast(I32))
+        nc.sync.dma_start(offsets[:], dst)
         nc.sync.dma_start(out=x_codes[:].bitcast(I32), in_=x_words[0].rearrange("p n t -> p (n t)").bitcast(I32))
         nc.sync.dma_start(out=gate_sb[:], in_=gate)
 
@@ -59,11 +58,11 @@ def tile_picked_wroute2_linnone_lo_kernel(tc, x_words, x_scales, gate, w1, dst, 
 
         w_view = w_grouped[:].rearrange("p (t m j) -> p m t j", t=PACK, j=PACK)
         raw_views = [raw[:].rearrange("p j (m t) -> p m t j", t=PACK) for raw in w_raw]
-        nc.scalar.copy(out=w_view[:, 0:32], in_=raw_views[0][:, 0:32])
-        nc.vector.tensor_copy(out=w_view[:, 32:64], in_=raw_views[0][:, 32:64])
-        nc.vector.tensor_copy(out=w_view[:, 64:96], in_=raw_views[1])
-        nc.scalar.copy(out=w_view[:, 96:128, 0], in_=raw_views[2][:, :, 0])
-        nc.vector.tensor_copy(out=w_view[:, 96:128, 1:4], in_=raw_views[2][:, :, 1:4])
+        nc.scalar.copy(out=w_view[:, 0:32, :, 0:2], in_=raw_views[0][:, 0:32])
+        nc.vector.tensor_copy(out=w_view[:, 32:128, :, 0:2], in_=raw_views[0][:, 32:128])
+        nc.vector.tensor_copy(out=w_view[:, :, first, 2:4], in_=raw_views[1][:, :, first])
+        nc.scalar.copy(out=w_view[:, :, last, 2:4], in_=raw_views[1][:, :, last])
+        nc.vector.tensor_copy(out=w_view[:, 0:64, 2:4, 2:4], in_=raw_views[1][:, 0:64, 2:4])
 
         def quantize_w(t0, t1):
             nc.vector.quantize_mx(
@@ -94,6 +93,7 @@ def tile_picked_wroute2_linnone_lo_kernel(tc, x_words, x_scales, gate, w1, dst, 
 
         quantize_w(first, first + 1)
         project(first, [(0, HEAD)], "acc_head")
+        nc.vector.tensor_copy(out=w_view[:, 64:128, 2:4, 2:4], in_=raw_views[1][:, 64:128, 2:4])
         quantize_w(last, last + 1)
         quantize_w(second, third + 1)
         project(first, [(HEAD, 2 * HEAD), (2 * HEAD, T)], "acc_first")

@@ -16,8 +16,15 @@ MULT = mybir.AluOpType.mult
 
 P = 128
 PACK = 4
-HEAD = 128
+QUADRANT = 32
+BLOCKS = 16
+PER_COLUMN = 16
 X_ROW = 4
+HEAD = 128
+SCALAR_M = 32
+CHUNK = 256
+
+FIRST, SECOND, THIRD, LAST = 0, 2, 3, 1
 
 
 def tile_picked_wroute2_linnone_lo_kernel(tc, x_words, x_scales, gate, w1, dst, out_0, out_1, out_2):
@@ -26,7 +33,7 @@ def tile_picked_wroute2_linnone_lo_kernel(tc, x_words, x_scales, gate, w1, dst, 
         keep = ctx.enter_context(tc.tile_pool(name="keep", bufs=1))
         psum = ctx.enter_context(tc.psum_pool(name="psum", bufs=1))
 
-        offsets = keep.tile([P, T // 16], U16, name="offsets")
+        offsets = keep.tile([P, T // PER_COLUMN], U16, name="offsets")
         x_codes = keep.tile([P, T], U32, name="x_codes", align_bytes=64)
         scales = keep.tile([P, T], U8, name="scales", align_bytes=64)
         gate_sb = keep.tile([P, T], F32, name="gate_sb")
@@ -34,35 +41,32 @@ def tile_picked_wroute2_linnone_lo_kernel(tc, x_words, x_scales, gate, w1, dst, 
         w_codes = keep.tile([P, N], U32, name="w_codes", align_bytes=64)
         y_grouped = keep.tile([P, U * PACK], BF16, name="y_grouped", align_bytes=64)
         y_codes = keep.tile([P, U], U32, name="y_codes", align_bytes=64)
-        y_plane = keep.tile([P, U], U8, name="y_plane", align_bytes=64)
+        y_scales = keep.tile([P, U], U8, name="y_scales", align_bytes=64)
         windows = [keep.tile([P, U], F32, name="window%d" % t) for t in range(PACK)]
         staged = [keep.tile([P, T], F32, name="staged%d" % t) for t in range(PACK)]
         w_raw = [keep.tile([P, 2, N], F32, name="w_raw%d" % u) for u in range(2)]
 
-        first, second, third, last = 0, 2, 3, 1
-
         w_rows = w1.rearrange("(p j) c -> p j c", j=PACK)
         for u in range(2):
             nc.sync.dma_start(out=w_raw[u][:], in_=w_rows[:, 2 * u : 2 * u + 2, :])
-        for q in range(4):
-            rows = slice(32 * q + X_ROW, 32 * q + X_ROW + 4)
-            nc.sync.dma_start(out=scales[rows, :].bitcast(I32), in_=x_scales[0][4 * q : 4 * q + 4, :].bitcast(I32))
+        for r in range(PACK):
+            nc.sync.dma_start(out=scales[X_ROW + r : P : QUADRANT, :].bitcast(I32), in_=x_scales[0][r:BLOCKS:PACK, :].bitcast(I32))
         nc.sync.dma_start(offsets[:], dst)
         nc.sync.dma_start(out=x_codes[:].bitcast(I32), in_=x_words[0].rearrange("p n t -> p (n t)").bitcast(I32))
         nc.sync.dma_start(out=gate_sb[:], in_=gate)
 
-        for t in (first, second, third, last)[:3]:
+        for t in (FIRST, SECOND, THIRD):
             nc.vector.memset(windows[t][:].bitcast(I32), 0)
-        for t in (first, second, third, last)[3:]:
-            nc.gpsimd.memset(windows[t][:].bitcast(I32), 0)
+        nc.gpsimd.memset(windows[LAST][:].bitcast(I32), 0)
 
         w_view = w_grouped[:].rearrange("p (t m j) -> p m t j", t=PACK, j=PACK)
-        raw_views = [raw[:].rearrange("p j (m t) -> p m t j", t=PACK) for raw in w_raw]
-        nc.scalar.copy(out=w_view[:, 0:32, :, 0:2], in_=raw_views[0][:, 0:32])
-        nc.vector.tensor_copy(out=w_view[:, 32:128, :, 0:2], in_=raw_views[0][:, 32:128])
-        nc.vector.tensor_copy(out=w_view[:, :, first, 2:4], in_=raw_views[1][:, :, first])
-        nc.scalar.copy(out=w_view[:, :, last, 2:4], in_=raw_views[1][:, :, last])
-        nc.vector.tensor_copy(out=w_view[:, 0:64, 2:4, 2:4], in_=raw_views[1][:, 0:64, 2:4])
+        rows_01, rows_23 = (raw[:].rearrange("p j (m t) -> p m t j", t=PACK) for raw in w_raw)
+        nc.scalar.copy(out=w_view[:, :SCALAR_M, :, 0:2], in_=rows_01[:, :SCALAR_M])
+        nc.vector.tensor_copy(out=w_view[:, SCALAR_M:, :, 0:2], in_=rows_01[:, SCALAR_M:])
+        middle = slice(SECOND, THIRD + 1)
+        nc.vector.tensor_copy(out=w_view[:, :, FIRST, 2:4], in_=rows_23[:, :, FIRST])
+        nc.scalar.copy(out=w_view[:, :, LAST, 2:4], in_=rows_23[:, :, LAST])
+        nc.vector.tensor_copy(out=w_view[:, : P // 2, middle, 2:4], in_=rows_23[:, : P // 2, middle])
 
         def quantize_w(t0, t1):
             nc.vector.quantize_mx(
@@ -87,48 +91,58 @@ def tile_picked_wroute2_linnone_lo_kernel(tc, x_words, x_scales, gate, w1, dst, 
             nc.scalar.copy(out=staged[t][:, lo:hi], in_=acc[:])
 
         def scatter(t, a, b):
-            nc.vector.tensor_tensor(
-                windows[t][:].indirect(offsets[:, a // 16 : b // 16]), staged[t][:, a:b], gate_sb[:, a:b], MULT
-            )
+            listed = offsets[:, a // PER_COLUMN : b // PER_COLUMN]
+            nc.vector.tensor_tensor(windows[t][:].indirect(listed), staged[t][:, a:b], gate_sb[:, a:b], MULT)
 
-        quantize_w(first, first + 1)
-        project(first, [(0, HEAD)], "acc_head")
-        nc.vector.tensor_copy(out=w_view[:, 64:128, 2:4, 2:4], in_=raw_views[1][:, 64:128, 2:4])
-        quantize_w(last, last + 1)
-        quantize_w(second, third + 1)
-        project(first, [(HEAD, 2 * HEAD), (2 * HEAD, T)], "acc_first")
-        for t in (second, third, last):
+        quantize_w(FIRST, FIRST + 1)
+        project(FIRST, [(0, HEAD)], "acc_head")
+        nc.vector.tensor_copy(out=w_view[:, P // 2 :, middle, 2:4], in_=rows_23[:, P // 2 :, middle])
+        quantize_w(LAST, LAST + 1)
+        quantize_w(SECOND, THIRD + 1)
+        project(FIRST, [(HEAD, 2 * HEAD), (2 * HEAD, T)], "acc_first")
+        for t in (SECOND, THIRD, LAST):
             project(t, [(0, T)], "acc%d" % t)
 
         out_rows = out_0.rearrange("(p t) c -> p t c", t=PACK)
         y_view = y_grouped[:].rearrange("p (c t) -> p c t", t=PACK)
+        chunks = [slice(a, a + CHUNK) for a in range(0, U, CHUNK)]
 
-        scatter(first, 0, HEAD)
-        scatter(first, HEAD, T)
-        nc.sync.dma_start(out=out_rows[:, first, :], in_=windows[first][:])
-        nc.scalar.copy(out=y_view[:, :, first : first + 2], in_=windows[first][:].unsqueeze(2).to_broadcast([P, U, 2]))
-        scatter(second, 0, T)
-        nc.sync.dma_start(out=out_rows[:, second, :], in_=windows[second][:])
-        nc.scalar.copy(out=y_view[:, :, second], in_=windows[second][:])
-        scatter(third, 0, T)
-        nc.sync.dma_start(out=out_rows[:, third, :], in_=windows[third][:])
-        for a, b in [[0,256],[256,512],[512,768],[768,1024]]:
-            nc.scalar.copy(out=y_view[:, a:b, third], in_=windows[third][:, a:b])
-        scatter(last, 0, T)
-        nc.sync.dma_start(out=out_rows[:, last, :], in_=windows[last][:])
-        nc.vector.tensor_copy(out=y_view[:, 0:256, last], in_=windows[last][:, 0:256])
-        nc.scalar.copy(out=y_view[:, 512:768, last], in_=windows[last][:, 512:768])
-        nc.vector.tensor_copy(out=y_view[:, 256:512, last], in_=windows[last][:, 256:512])
-        nc.scalar.copy(out=y_view[:, 768:1024, last], in_=windows[last][:, 768:1024])
+        scatter(FIRST, 0, HEAD)
+        scatter(FIRST, HEAD, T)
+        nc.sync.dma_start(out=out_rows[:, FIRST, :], in_=windows[FIRST][:])
+        nc.scalar.copy(out=y_view[:, :, FIRST : LAST + 1], in_=windows[FIRST][:].unsqueeze(2).to_broadcast([P, U, 2]))
+        scatter(SECOND, 0, T)
+        nc.sync.dma_start(out=out_rows[:, SECOND, :], in_=windows[SECOND][:])
+        nc.scalar.copy(out=y_view[:, :, SECOND], in_=windows[SECOND][:])
+        scatter(THIRD, 0, T)
+        nc.sync.dma_start(out=out_rows[:, THIRD, :], in_=windows[THIRD][:])
+        for cols in chunks:
+            nc.scalar.copy(out=y_view[:, cols, THIRD], in_=windows[THIRD][:, cols])
+        scatter(LAST, 0, T)
+        nc.sync.dma_start(out=out_rows[:, LAST, :], in_=windows[LAST][:])
 
-        words_out = out_1[0].rearrange("p n t -> p (n t)").bitcast(I32)
-        for a, b in [[0,256],[256,512],[512,768],[768,1024]]:
+        half = len(chunks) // 2
+        for mine, other in zip(chunks[:half], chunks[half:]):
+            nc.vector.tensor_copy(out=y_view[:, mine, LAST], in_=windows[LAST][:, mine])
+            nc.scalar.copy(out=y_view[:, other, LAST], in_=windows[LAST][:, other])
+
+        def quantize_y(cols):
             nc.vector.quantize_mx(
-                out=y_codes[:, a:b].bitcast(FP8X4), scales=y_plane[:, a:b], in_=y_grouped[:, PACK * a : PACK * b]
+                out=y_codes[:, cols].bitcast(FP8X4),
+                scales=y_scales[:, cols],
+                in_=y_grouped[:, PACK * cols.start : PACK * cols.stop],
             )
-            if b in {512: 0, 768: 512, 1024: 768}:
-                a = {512: 0, 768: 512, 1024: 768}[b]
-                nc.sync.dma_start(out=words_out[:, a:b], in_=y_codes[:, a:b].bitcast(I32))
-        for q in range(4):
-            queue = nc.sync if q % 2 else nc.scalar
-            queue.dma_start(out=out_2[0][4 * q : 4 * q + 4, :].bitcast(I32), in_=y_plane[32 * q : 32 * q + 4, :].bitcast(I32))
+
+        def store_words(cols):
+            words_out = out_1[0].rearrange("p n t -> p (n t)").bitcast(I32)
+            nc.sync.dma_start(out=words_out[:, cols], in_=y_codes[:, cols].bitcast(I32))
+
+        for cols in chunks[:half]:
+            quantize_y(cols)
+        store_words(slice(0, U // 2))
+        for cols in chunks[half:]:
+            quantize_y(cols)
+            store_words(cols)
+        for r in range(PACK):
+            queue = nc.sync if r % 2 else nc.scalar
+            queue.dma_start(out=out_2[0][r:BLOCKS:PACK, :].bitcast(I32), in_=y_scales[r:P:QUADRANT, :].bitcast(I32))

@@ -55,9 +55,8 @@ def tile_picked_wroute2_linnone_lo_kernel(tc, x_words, x_scales, gate, w1, dst, 
         nc.sync.dma_start(out=x_codes[:].bitcast(I32), in_=x_words[0].rearrange("p n t -> p (n t)").bitcast(I32))
         nc.sync.dma_start(out=gate_sb[:], in_=gate)
 
-        for t in (FIRST, SECOND, THIRD):
+        for t in (FIRST, SECOND, THIRD, LAST):
             nc.vector.memset(windows[t][:].bitcast(I32), 0)
-        nc.gpsimd.memset(windows[LAST][:].bitcast(I32), 0)
 
         w_view = w_grouped[:].rearrange("p (t m j) -> p m t j", t=PACK, j=PACK)
         rows_01, rows_23 = (raw[:].rearrange("p j (m t) -> p m t j", t=PACK) for raw in w_raw)
@@ -110,14 +109,15 @@ def tile_picked_wroute2_linnone_lo_kernel(tc, x_words, x_scales, gate, w1, dst, 
         scatter(FIRST, 0, HEAD)
         scatter(FIRST, HEAD, T)
         nc.sync.dma_start(out=out_rows[:, FIRST, :], in_=windows[FIRST][:])
-        nc.scalar.copy(out=y_view[:, :, FIRST : LAST + 1], in_=windows[FIRST][:].unsqueeze(2).to_broadcast([P, U, 2]))
+        twice = windows[FIRST][:, : U // 2].unsqueeze(2).to_broadcast([P, U // 2, 2])
+        nc.scalar.copy(out=y_view[:, : U // 2, FIRST : LAST + 1], in_=twice)
+        nc.scalar.copy(out=y_view[:, U // 2 :, FIRST], in_=windows[FIRST][:, U // 2 :])
         scatter(SECOND, 0, T)
         nc.sync.dma_start(out=out_rows[:, SECOND, :], in_=windows[SECOND][:])
         nc.scalar.copy(out=y_view[:, :, SECOND], in_=windows[SECOND][:])
         scatter(THIRD, 0, T)
         nc.sync.dma_start(out=out_rows[:, THIRD, :], in_=windows[THIRD][:])
-        for cols in chunks:
-            nc.scalar.copy(out=y_view[:, cols, THIRD], in_=windows[THIRD][:, cols])
+        nc.scalar.copy(out=y_view[:, :, THIRD], in_=windows[THIRD][:])
         scatter(LAST, 0, T)
         nc.sync.dma_start(out=out_rows[:, LAST, :], in_=windows[LAST][:])
 

@@ -44,6 +44,7 @@ def tile_picked_wroute2_linnone_lo_kernel(tc, x_words, x_scales, gate, w1, dst, 
         y_scales = keep.tile([P, U], U8, name="y_scales", align_bytes=64)
         windows = [keep.tile([P, U], F32, name="window%d" % t) for t in range(PACK)]
         staged = [keep.tile([P, T], F32, name="staged%d" % t) for t in range(PACK)]
+        plain = {t: keep.tile([P, T], F32, name="plain%d" % t) for t in (SECOND, THIRD, LAST)}
         w_raw = [keep.tile([P, 2, N], F32, name="w_raw%d" % u) for u in range(2)]
 
         w_rows = w1.rearrange("(p j) c -> p j c", j=PACK)
@@ -87,11 +88,15 @@ def tile_picked_wroute2_linnone_lo_kernel(tc, x_words, x_scales, gate, w1, dst, 
                     start=True,
                     stop=True,
                 )
-            nc.scalar.copy(out=staged[t][:, lo:hi], in_=acc[:])
+            if t == FIRST:
+                nc.vector.tensor_tensor(staged[t][:, lo:hi], acc[:], gate_sb[:, lo:hi], MULT)
+            else:
+                nc.scalar.copy(out=plain[t][:, lo:hi], in_=acc[:])
+                nc.gpsimd.tensor_tensor(staged[t][:, lo:hi], plain[t][:, lo:hi], gate_sb[:, lo:hi], MULT)
 
         def scatter(t, a, b):
             listed = offsets[:, a // PER_COLUMN : b // PER_COLUMN]
-            nc.vector.tensor_tensor(windows[t][:].indirect(listed), staged[t][:, a:b], gate_sb[:, a:b], MULT)
+            nc.vector.tensor_copy(windows[t][:].indirect(listed), staged[t][:, a:b])
 
         quantize_w(FIRST, FIRST + 1)
         project(FIRST, [(0, HEAD)], "acc_head")

@@ -13,6 +13,7 @@ U16 = mybir.dt.uint16
 U8 = mybir.dt.uint8
 FP8X4 = mybir.dt.float8_e4m3fn_x4
 MULT = mybir.AluOpType.mult
+ADD = mybir.AluOpType.add
 
 P = 128
 PACK = 4
@@ -20,11 +21,10 @@ QUADRANT = 32
 BLOCKS = 16
 PER_COLUMN = 16
 X_ROW = 4
-HEAD = 128
+PIECES = [(0, 128), (128, 256), (256, 512)]
 SCALAR_M = 32
 CHUNK = 256
-
-FIRST, SECOND, THIRD, LAST = 0, 2, 3, 1
+SPLIT = U // 2
 
 
 def tile_picked_wroute2_linnone_lo_kernel(tc, x_words, x_scales, gate, w1, dst, out_0, out_1, out_2):
@@ -43,30 +43,29 @@ def tile_picked_wroute2_linnone_lo_kernel(tc, x_words, x_scales, gate, w1, dst, 
         y_codes = keep.tile([P, U], U32, name="y_codes", align_bytes=64)
         y_scales = keep.tile([P, U], U8, name="y_scales", align_bytes=64)
         windows = [keep.tile([P, U], F32, name="window%d" % t) for t in range(PACK)]
-        staged = [keep.tile([P, T], F32, name="staged%d" % t) for t in range(PACK)]
-        plain = {t: keep.tile([P, T], F32, name="plain%d" % t) for t in (SECOND, THIRD, LAST)}
+        plain = [keep.tile([P, T], F32, name="plain%d" % t) for t in range(PACK)]
+        gated = [keep.tile([P, T], F32, name="gated%d" % t) for t in range(PACK)]
         w_raw = [keep.tile([P, 2, N], F32, name="w_raw%d" % u) for u in range(2)]
 
+        for r in range(PACK):
+            nc.scalar.dma_start(out=scales[X_ROW + r : P : QUADRANT, :].bitcast(I32), in_=x_scales[0][r:BLOCKS:PACK, :].bitcast(I32))
         w_rows = w1.rearrange("(p j) c -> p j c", j=PACK)
         for u in range(2):
             nc.sync.dma_start(out=w_raw[u][:], in_=w_rows[:, 2 * u : 2 * u + 2, :])
-        for r in range(PACK):
-            nc.sync.dma_start(out=scales[X_ROW + r : P : QUADRANT, :].bitcast(I32), in_=x_scales[0][r:BLOCKS:PACK, :].bitcast(I32))
-        nc.sync.dma_start(offsets[:], dst)
         nc.sync.dma_start(out=x_codes[:].bitcast(I32), in_=x_words[0].rearrange("p n t -> p (n t)").bitcast(I32))
         nc.sync.dma_start(out=gate_sb[:], in_=gate)
+        nc.sync.dma_start(offsets[:], dst)
 
-        for t in (FIRST, SECOND, THIRD, LAST):
+        for t in range(PACK):
             nc.vector.memset(windows[t][:].bitcast(I32), 0)
 
         w_view = w_grouped[:].rearrange("p (t m j) -> p m t j", t=PACK, j=PACK)
         rows_01, rows_23 = (raw[:].rearrange("p j (m t) -> p m t j", t=PACK) for raw in w_raw)
         nc.scalar.copy(out=w_view[:, :SCALAR_M, :, 0:2], in_=rows_01[:, :SCALAR_M])
         nc.vector.tensor_copy(out=w_view[:, SCALAR_M:, :, 0:2], in_=rows_01[:, SCALAR_M:])
-        middle = slice(SECOND, THIRD + 1)
-        nc.vector.tensor_copy(out=w_view[:, :, FIRST, 2:4], in_=rows_23[:, :, FIRST])
-        nc.scalar.copy(out=w_view[:, :, LAST, 2:4], in_=rows_23[:, :, LAST])
-        nc.vector.tensor_copy(out=w_view[:, : P // 2, middle, 2:4], in_=rows_23[:, : P // 2, middle])
+        nc.vector.tensor_copy(out=w_view[:, :, 0, 2:4], in_=rows_23[:, :, 0])
+        nc.scalar.copy(out=w_view[:, :, 2:4, 2:4], in_=rows_23[:, :, 2:4])
+        nc.vector.tensor_copy(out=w_view[:, :, 1, 2:4], in_=rows_23[:, :, 1])
 
         def quantize_w(t0, t1):
             nc.vector.quantize_mx(
@@ -75,61 +74,68 @@ def tile_picked_wroute2_linnone_lo_kernel(tc, x_words, x_scales, gate, w1, dst, 
                 in_=w_grouped[:, PACK * P * t0 : PACK * P * t1],
             )
 
-        def project(t, pieces, name):
-            lo, hi = pieces[0][0], pieces[-1][1]
-            acc = psum.tile([P, hi - lo], F32, name=name)
-            for a, b in pieces:
-                nc.tensor.matmul_mx(
-                    out=acc[:, a - lo : b - lo],
-                    lhsT=w_codes[:, P * t : P * (t + 1)].bitcast(FP8X4),
-                    lhsT_scale=scales[:, P * t : P * (t + 1)],
-                    rhs=x_codes[:, a:b].bitcast(FP8X4),
-                    rhs_scale=scales[X_ROW:P, a:b],
-                    start=True,
-                    stop=True,
-                )
-            if t == FIRST:
-                nc.vector.tensor_tensor(staged[t][:, lo:hi], acc[:], gate_sb[:, lo:hi], MULT)
-            else:
-                nc.scalar.copy(out=plain[t][:, lo:hi], in_=acc[:])
-                nc.gpsimd.tensor_tensor(staged[t][:, lo:hi], plain[t][:, lo:hi], gate_sb[:, lo:hi], MULT)
+        def project(t, a, b):
+            acc = psum.tile([P, b - a], F32, name="acc%d_%d" % (t, a))
+            nc.tensor.matmul_mx(
+                out=acc[:],
+                lhsT=w_codes[:, P * t : P * (t + 1)].bitcast(FP8X4),
+                lhsT_scale=scales[:, P * t : P * (t + 1)],
+                rhs=x_codes[:, a:b].bitcast(FP8X4),
+                rhs_scale=scales[X_ROW:P, a:b],
+                start=True,
+                stop=True,
+            )
+            return acc
+
+        def gate_on_gpsimd(t, a, b):
+            nc.scalar.copy(out=plain[t][:, a:b], in_=project(t, a, b)[:])
+            nc.gpsimd.tensor_tensor(gated[t][:, a:b], plain[t][:, a:b], gate_sb[:, a:b], MULT)
 
         def scatter(t, a, b):
             listed = offsets[:, a // PER_COLUMN : b // PER_COLUMN]
-            nc.vector.tensor_copy(windows[t][:].indirect(listed), staged[t][:, a:b])
+            nc.vector.tensor_copy(windows[t][:].indirect(listed), gated[t][:, a:b])
 
-        quantize_w(FIRST, FIRST + 1)
-        project(FIRST, [(0, HEAD)], "acc_head")
-        nc.vector.tensor_copy(out=w_view[:, P // 2 :, middle, 2:4], in_=rows_23[:, P // 2 :, middle])
-        quantize_w(LAST, LAST + 1)
-        quantize_w(SECOND, THIRD + 1)
-        project(FIRST, [(HEAD, 2 * HEAD), (2 * HEAD, T)], "acc_first")
-        for t in (SECOND, THIRD, LAST):
-            project(t, [(0, T)], "acc%d" % t)
+        quantize_w(0, 1)
+        a, b = PIECES[0]
+        first = project(0, a, b)
+        quantize_w(1, 2)
+        nc.vector.tensor_tensor(gated[0][:, a:b], first[:], gate_sb[:, a:b], MULT)
+        gate_on_gpsimd(1, a, b)
+        gate_on_gpsimd(0, *PIECES[1])
+        gate_on_gpsimd(1, *PIECES[1])
+        quantize_w(2, 4)
+        gate_on_gpsimd(0, *PIECES[2])
+        gate_on_gpsimd(1, *PIECES[2])
+        for t in (2, 3):
+            gate_on_gpsimd(t, 0, T)
 
         out_rows = out_0.rearrange("(p t) c -> p t c", t=PACK)
         y_view = y_grouped[:].rearrange("p (c t) -> p c t", t=PACK)
         chunks = [slice(a, a + CHUNK) for a in range(0, U, CHUNK)]
+        low, high = slice(0, SPLIT), slice(SPLIT, U)
 
-        scatter(FIRST, 0, HEAD)
-        scatter(FIRST, HEAD, T)
-        nc.sync.dma_start(out=out_rows[:, FIRST, :], in_=windows[FIRST][:])
-        twice = windows[FIRST][:, : U // 2].unsqueeze(2).to_broadcast([P, U // 2, 2])
-        nc.scalar.copy(out=y_view[:, : U // 2, FIRST : LAST + 1], in_=twice)
-        nc.scalar.copy(out=y_view[:, U // 2 :, FIRST], in_=windows[FIRST][:, U // 2 :])
-        scatter(SECOND, 0, T)
-        nc.sync.dma_start(out=out_rows[:, SECOND, :], in_=windows[SECOND][:])
-        nc.scalar.copy(out=y_view[:, :, SECOND], in_=windows[SECOND][:])
-        scatter(THIRD, 0, T)
-        nc.sync.dma_start(out=out_rows[:, THIRD, :], in_=windows[THIRD][:])
-        nc.scalar.copy(out=y_view[:, :, THIRD], in_=windows[THIRD][:])
-        scatter(LAST, 0, T)
-        nc.sync.dma_start(out=out_rows[:, LAST, :], in_=windows[LAST][:])
+        def weave(t, width):
+            def source(cols):
+                return windows[t][:, cols].unsqueeze(2).to_broadcast([P, cols.stop - cols.start, width])
+
+            nc.sync.dma_start(out=out_rows[:, t, :], in_=windows[t][:])
+            nc.scalar.copy(out=y_view[:, low, t : t + width], in_=source(low))
+            nc.gpsimd.tensor_scalar(y_view[:, high, t : t + width], source(high), 1.0, 0.0, MULT, ADD)
+
+        for a, b in PIECES:
+            scatter(0, a, b)
+            scatter(1, a, b)
+        weave(0, 1)
+        weave(1, 1)
+        scatter(2, 0, T)
+        weave(2, 2)
+        scatter(3, 0, T)
+        nc.sync.dma_start(out=out_rows[:, 3, :], in_=windows[3][:])
 
         half = len(chunks) // 2
         for mine, other in zip(chunks[:half], chunks[half:]):
-            nc.vector.tensor_copy(out=y_view[:, mine, LAST], in_=windows[LAST][:, mine])
-            nc.scalar.copy(out=y_view[:, other, LAST], in_=windows[LAST][:, other])
+            nc.vector.tensor_copy(out=y_view[:, mine, 3], in_=windows[3][:, mine])
+            nc.scalar.copy(out=y_view[:, other, 3], in_=windows[3][:, other])
 
         def quantize_y(cols):
             nc.vector.quantize_mx(

@@ -20,7 +20,6 @@ PACK = 4
 QUADRANT = 32
 BLOCKS = 16
 PER_COLUMN = 16
-X_ROW = 4
 PIECES = [(0, 128), (128, 256), (256, 512)]
 SCALAR_M = 32
 CHUNK = 256
@@ -35,26 +34,29 @@ def tile_picked_wroute2_linnone_lo_kernel(tc, x_words, x_scales, gate, w1, dst, 
 
         offsets = keep.tile([P, T // PER_COLUMN], U16, name="offsets")
         x_codes = keep.tile([P, T], U32, name="x_codes", align_bytes=64)
-        scales = keep.tile([P, T], U8, name="scales", align_bytes=64)
+        x_plane = keep.tile([P, T], U8, name="x_plane", align_bytes=64)
+        w_plane = keep.tile([P, N], U8, name="w_plane", align_bytes=64)
         gate_sb = keep.tile([P, T], F32, name="gate_sb")
         w_grouped = keep.tile([P, N * PACK], BF16, name="w_grouped", align_bytes=64)
         w_codes = keep.tile([P, N], U32, name="w_codes", align_bytes=64)
-        y_grouped = keep.tile([P, U * PACK], BF16, name="y_grouped", align_bytes=64)
         y_codes = keep.tile([P, U], U32, name="y_codes", align_bytes=64)
         y_scales = keep.tile([P, U], U8, name="y_scales", align_bytes=64)
         windows = [keep.tile([P, U], F32, name="window%d" % t) for t in range(PACK)]
-        plain = [keep.tile([P, T], F32, name="plain%d" % t) for t in range(PACK)]
+        plain = [keep.tile([P, T], F32, name="plain%d" % t, align_bytes=64) for t in range(PACK)]
         gated = [keep.tile([P, T], F32, name="gated%d" % t) for t in range(PACK)]
         w_raw = [keep.tile([P, 2, N], F32, name="w_raw%d" % u) for u in range(2)]
 
-        for r in range(PACK):
-            nc.scalar.dma_start(out=scales[X_ROW + r : P : QUADRANT, :].bitcast(I32), in_=x_scales[0][r:BLOCKS:PACK, :].bitcast(I32))
         w_rows = w1.rearrange("(p j) c -> p j c", j=PACK)
+        x_rows = x_words[0].rearrange("p n t -> p (n t)").bitcast(I32)
         for u in range(2):
             nc.sync.dma_start(out=w_raw[u][:], in_=w_rows[:, 2 * u : 2 * u + 2, :])
-        nc.sync.dma_start(out=x_codes[:].bitcast(I32), in_=x_words[0].rearrange("p n t -> p (n t)").bitcast(I32))
-        nc.sync.dma_start(out=gate_sb[:], in_=gate)
+        for r in range(PACK):
+            nc.sync.dma_start(out=x_plane[r:P:QUADRANT, :].bitcast(I32), in_=x_scales[0][r:BLOCKS:PACK, :].bitcast(I32))
+        nc.sync.dma_start(out=x_codes[:, : T // 2].bitcast(I32), in_=x_rows[:, : T // 2])
+        nc.sync.dma_start(out=gate_sb[:, : T // 2], in_=gate[:, : T // 2])
         nc.sync.dma_start(offsets[:], dst)
+        nc.sync.dma_start(out=x_codes[:, T // 2 :].bitcast(I32), in_=x_rows[:, T // 2 :])
+        nc.sync.dma_start(out=gate_sb[:, T // 2 :], in_=gate[:, T // 2 :])
 
         for t in range(PACK):
             nc.vector.memset(windows[t][:].bitcast(I32), 0)
@@ -64,13 +66,13 @@ def tile_picked_wroute2_linnone_lo_kernel(tc, x_words, x_scales, gate, w1, dst, 
         nc.scalar.copy(out=w_view[:, :SCALAR_M, :, 0:2], in_=rows_01[:, :SCALAR_M])
         nc.vector.tensor_copy(out=w_view[:, SCALAR_M:, :, 0:2], in_=rows_01[:, SCALAR_M:])
         nc.vector.tensor_copy(out=w_view[:, :, 0, 2:4], in_=rows_23[:, :, 0])
-        nc.scalar.copy(out=w_view[:, :, 2:4, 2:4], in_=rows_23[:, :, 2:4])
+        nc.scalar.copy(out=w_view[:, :, 3, 2:4], in_=rows_23[:, :, 3])
         nc.vector.tensor_copy(out=w_view[:, :, 1, 2:4], in_=rows_23[:, :, 1])
 
         def quantize_w(t0, t1):
             nc.vector.quantize_mx(
                 out=w_codes[:, P * t0 : P * t1].bitcast(FP8X4),
-                scales=scales[:, P * t0 : P * t1],
+                scales=w_plane[:, P * t0 : P * t1],
                 in_=w_grouped[:, PACK * P * t0 : PACK * P * t1],
             )
 
@@ -79,9 +81,9 @@ def tile_picked_wroute2_linnone_lo_kernel(tc, x_words, x_scales, gate, w1, dst, 
             nc.tensor.matmul_mx(
                 out=acc[:],
                 lhsT=w_codes[:, P * t : P * (t + 1)].bitcast(FP8X4),
-                lhsT_scale=scales[:, P * t : P * (t + 1)],
+                lhsT_scale=w_plane[:, P * t : P * (t + 1)],
                 rhs=x_codes[:, a:b].bitcast(FP8X4),
-                rhs_scale=scales[X_ROW:P, a:b],
+                rhs_scale=x_plane[:, a:b],
                 start=True,
                 stop=True,
             )
@@ -98,6 +100,7 @@ def tile_picked_wroute2_linnone_lo_kernel(tc, x_words, x_scales, gate, w1, dst, 
         quantize_w(0, 1)
         a, b = PIECES[0]
         first = project(0, a, b)
+        nc.vector.tensor_copy(out=w_view[:, :, 2, 2:4], in_=rows_23[:, :, 2])
         quantize_w(1, 2)
         nc.vector.tensor_tensor(gated[0][:, a:b], first[:], gate_sb[:, a:b], MULT)
         gate_on_gpsimd(1, a, b)
@@ -109,6 +112,7 @@ def tile_picked_wroute2_linnone_lo_kernel(tc, x_words, x_scales, gate, w1, dst, 
         for t in (2, 3):
             gate_on_gpsimd(t, 0, T)
 
+        y_grouped = keep.tile([P, U * PACK], BF16, name="y_grouped", tag="plain3", align_bytes=64)
         out_rows = out_0.rearrange("(p t) c -> p t c", t=PACK)
         y_view = y_grouped[:].rearrange("p (c t) -> p c t", t=PACK)
         chunks = [slice(a, a + CHUNK) for a in range(0, U, CHUNK)]

@@ -21,9 +21,9 @@ QUADRANT = 32
 BLOCKS = 16
 PER_COLUMN = 16
 PIECES = [(0, 128), (128, 256), (256, 512)]
-SCALAR_M = 32
+SCALAR_M = 64
 CHUNK = 256
-SPLIT = U // 2
+SPLIT = 576
 
 
 def tile_picked_wroute2_linnone_lo_kernel(tc, x_words, x_scales, gate, w1, dst, out_0, out_1, out_2):
@@ -103,7 +103,7 @@ def tile_picked_wroute2_linnone_lo_kernel(tc, x_words, x_scales, gate, w1, dst, 
         nc.vector.tensor_copy(out=w_view[:, :, 2, 2:4], in_=rows_23[:, :, 2])
         quantize_w(1, 2)
         nc.vector.tensor_tensor(gated[0][:, a:b], first[:], gate_sb[:, a:b], MULT)
-        gate_on_gpsimd(1, a, b)
+        nc.vector.tensor_tensor(gated[1][:, a:b], project(1, a, b)[:], gate_sb[:, a:b], MULT)
         gate_on_gpsimd(0, *PIECES[1])
         gate_on_gpsimd(1, *PIECES[1])
         quantize_w(2, 4)
@@ -137,7 +137,7 @@ def tile_picked_wroute2_linnone_lo_kernel(tc, x_words, x_scales, gate, w1, dst, 
         nc.sync.dma_start(out=out_rows[:, 3, :], in_=windows[3][:])
 
         half = len(chunks) // 2
-        for mine, other in zip(chunks[:half], chunks[half:]):
+        for mine, other in ((slice(0, CHUNK), slice(SPLIT, U - CHUNK)), (slice(CHUNK, SPLIT), slice(U - CHUNK, U))):
             nc.vector.tensor_copy(out=y_view[:, mine, 3], in_=windows[3][:, mine])
             nc.scalar.copy(out=y_view[:, other, 3], in_=windows[3][:, other])
 
@@ -152,12 +152,10 @@ def tile_picked_wroute2_linnone_lo_kernel(tc, x_words, x_scales, gate, w1, dst, 
             words_out = out_1[0].rearrange("p n t -> p (n t)").bitcast(I32)
             nc.sync.dma_start(out=words_out[:, cols], in_=y_codes[:, cols].bitcast(I32))
 
-        for cols in chunks[:half]:
-            quantize_y(cols)
-        store_words(slice(0, U // 2))
-        for cols in chunks[half:]:
-            quantize_y(cols)
-            store_words(cols)
+        for group in ((0,256,384,),(384,512,768,),(768,1024,),):
+            for a, b in zip(group, group[1:]):
+                quantize_y(slice(a, b))
+            store_words(slice(group[0], group[-1]))
         for r in range(PACK):
             queue = nc.sync if r % 2 else nc.scalar
             queue.dma_start(out=out_2[0][r:BLOCKS:PACK, :].bitcast(I32), in_=y_scales[r:P:QUADRANT, :].bitcast(I32))

@@ -66,7 +66,8 @@ def tile_picked_wroute2_linnone_lo_kernel(tc, x_words, x_scales, gate, w1, dst, 
         nc.scalar.copy(out=w_view[:, :SCALAR_M, :, 0:2], in_=rows_01[:, :SCALAR_M])
         nc.vector.tensor_copy(out=w_view[:, SCALAR_M:, :, 0:2], in_=rows_01[:, SCALAR_M:])
         nc.vector.tensor_copy(out=w_view[:, :, 0, 2:4], in_=rows_23[:, :, 0])
-        nc.scalar.copy(out=w_view[:, :, 3, 2:4], in_=rows_23[:, :, 3])
+        for t in (2, 3):
+            nc.scalar.copy(out=w_view[:, :, t, 2:4], in_=rows_23[:, :, t])
         nc.vector.tensor_copy(out=w_view[:, :, 1, 2:4], in_=rows_23[:, :, 1])
 
         def quantize_w(t0, t1):
@@ -100,13 +101,12 @@ def tile_picked_wroute2_linnone_lo_kernel(tc, x_words, x_scales, gate, w1, dst, 
         quantize_w(0, 1)
         a, b = PIECES[0]
         first = project(0, a, b)
-        nc.vector.tensor_copy(out=w_view[:, :, 2, 2:4], in_=rows_23[:, :, 2])
-        quantize_w(1, 2)
+        for t in range(1, PACK):
+            quantize_w(t, t + 1)
         nc.vector.tensor_tensor(gated[0][:, a:b], first[:], gate_sb[:, a:b], MULT)
         nc.vector.tensor_tensor(gated[1][:, a:b], project(1, a, b)[:], gate_sb[:, a:b], MULT)
         gate_on_gpsimd(0, *PIECES[1])
         gate_on_gpsimd(1, *PIECES[1])
-        quantize_w(2, 4)
         gate_on_gpsimd(0, *PIECES[2])
         gate_on_gpsimd(1, *PIECES[2])
         for t in (2, 3):

@@ -23,7 +23,7 @@ PER_COLUMN = 16
 PIECES = [(0, 128), (128, 256), (256, 512)]
 SCALAR_M = 64
 CHUNK = 256
-SPLIT = 576
+SPLIT = 528
 
 
 def tile_picked_wroute2_linnone_lo_kernel(tc, x_words, x_scales, gate, w1, dst, out_0, out_1, out_2):
@@ -66,8 +66,7 @@ def tile_picked_wroute2_linnone_lo_kernel(tc, x_words, x_scales, gate, w1, dst, 
         nc.scalar.copy(out=w_view[:, :SCALAR_M, :, 0:2], in_=rows_01[:, :SCALAR_M])
         nc.vector.tensor_copy(out=w_view[:, SCALAR_M:, :, 0:2], in_=rows_01[:, SCALAR_M:])
         nc.vector.tensor_copy(out=w_view[:, :, 0, 2:4], in_=rows_23[:, :, 0])
-        for t in (2, 3):
-            nc.scalar.copy(out=w_view[:, :, t, 2:4], in_=rows_23[:, :, t])
+        nc.scalar.copy(out=w_view[:, :, 2:4, 2:4], in_=rows_23[:, :, 2:4])
         nc.vector.tensor_copy(out=w_view[:, :, 1, 2:4], in_=rows_23[:, :, 1])
 
         def quantize_w(t0, t1):
@@ -101,8 +100,8 @@ def tile_picked_wroute2_linnone_lo_kernel(tc, x_words, x_scales, gate, w1, dst, 
         quantize_w(0, 1)
         a, b = PIECES[0]
         first = project(0, a, b)
-        for t in range(1, PACK):
-            quantize_w(t, t + 1)
+        quantize_w(1, 2)
+        quantize_w(2, PACK)
         nc.vector.tensor_tensor(gated[0][:, a:b], first[:], gate_sb[:, a:b], MULT)
         nc.vector.tensor_tensor(gated[1][:, a:b], project(1, a, b)[:], gate_sb[:, a:b], MULT)
         gate_on_gpsimd(0, *PIECES[1])
@@ -124,7 +123,7 @@ def tile_picked_wroute2_linnone_lo_kernel(tc, x_words, x_scales, gate, w1, dst, 
 
             nc.sync.dma_start(out=out_rows[:, t, :], in_=windows[t][:])
             nc.scalar.copy(out=y_view[:, low, t : t + width], in_=source(low))
-            nc.gpsimd.tensor_scalar(y_view[:, high, t : t + width], source(high), 1.0, 0.0, MULT, ADD)
+            nc.gpsimd.tensor_scalar(y_view[:, high, t : t + width], source(high), 1.0, -0.0, MULT, ADD)
 
         for a, b in PIECES:
             scatter(0, a, b)

@@ -48,10 +48,10 @@ def tile_picked_wroute2_linnone_lo_kernel(tc, x_words, x_scales, gate, w1, dst, 
 
         w_rows = w1.rearrange("(p j) c -> p j c", j=PACK)
         x_rows = x_words[0].rearrange("p n t -> p (n t)").bitcast(I32)
-        for u in range(2):
-            nc.sync.dma_start(out=w_raw[u][:], in_=w_rows[:, 2 * u : 2 * u + 2, :])
+        nc.sync.dma_start(out=w_raw[0][:], in_=w_rows[:, 0:2, :])
         for r in range(PACK):
             nc.sync.dma_start(out=x_plane[r:P:QUADRANT, :].bitcast(I32), in_=x_scales[0][r:BLOCKS:PACK, :].bitcast(I32))
+        nc.sync.dma_start(out=w_raw[1][:], in_=w_rows[:, 2:4, :])
         nc.sync.dma_start(out=x_codes[:, : T // 2].bitcast(I32), in_=x_rows[:, : T // 2])
         nc.sync.dma_start(out=gate_sb[:, : T // 2], in_=gate[:, : T // 2])
         nc.sync.dma_start(offsets[:], dst)

@@ -14,16 +14,17 @@ U8 = mybir.dt.uint8
 FP8X4 = mybir.dt.float8_e4m3fn_x4
 MULT = mybir.AluOpType.mult
 ADD = mybir.AluOpType.add
+COPY = mybir.ActivationFunctionType.Copy
 
 P = 128
 PACK = 4
 QUADRANT = 32
 BLOCKS = 16
 PER_COLUMN = 16
-PIECES = [(0, 128), (128, 256), (256, 512)]
 SCALAR_M = 64
 CHUNK = 256
-SPLIT = 528
+SCALAR_PART = 192
+FIRST = 128
 
 
 def tile_picked_wroute2_linnone_lo_kernel(tc, x_words, x_scales, gate, w1, dst, out_0, out_1, out_2):
@@ -42,7 +43,8 @@ def tile_picked_wroute2_linnone_lo_kernel(tc, x_words, x_scales, gate, w1, dst, 
         y_codes = keep.tile([P, U], U32, name="y_codes", align_bytes=64)
         y_scales = keep.tile([P, U], U8, name="y_scales", align_bytes=64)
         windows = [keep.tile([P, U], F32, name="window%d" % t) for t in range(PACK)]
-        plain = [keep.tile([P, T], F32, name="plain%d" % t, align_bytes=64) for t in range(PACK)]
+        pairs = keep.tile([P, U * PACK], BF16, name="pairs", align_bytes=64)
+        y_grouped = keep.tile([P, U * PACK], BF16, name="y_grouped", align_bytes=64)
         gated = [keep.tile([P, T], F32, name="gated%d" % t) for t in range(PACK)]
         w_raw = [keep.tile([P, 2, N], F32, name="w_raw%d" % u) for u in range(2)]
 
@@ -78,67 +80,76 @@ def tile_picked_wroute2_linnone_lo_kernel(tc, x_words, x_scales, gate, w1, dst, 
 
         def project(t, a, b):
             acc = psum.tile([P, b - a], F32, name="acc%d_%d" % (t, a))
-            nc.tensor.matmul_mx(
-                out=acc[:],
-                lhsT=w_codes[:, P * t : P * (t + 1)].bitcast(FP8X4),
-                lhsT_scale=w_plane[:, P * t : P * (t + 1)],
-                rhs=x_codes[:, a:b].bitcast(FP8X4),
-                rhs_scale=x_plane[:, a:b],
-                start=True,
-                stop=True,
-            )
+            for lo, hi in ((a, b),) if (b - a) != 384 else ((a, a + 128), (a + 128, b)):
+                nc.tensor.matmul_mx(
+                    out=acc[:, lo - a : hi - a],
+                    lhsT=w_codes[:, P * t : P * (t + 1)].bitcast(FP8X4),
+                    lhsT_scale=w_plane[:, P * t : P * (t + 1)],
+                    rhs=x_codes[:, lo:hi].bitcast(FP8X4),
+                    rhs_scale=x_plane[:, lo:hi],
+                    start=True,
+                    stop=True,
+                )
             return acc
 
-        def gate_on_gpsimd(t, a, b):
-            nc.scalar.copy(out=plain[t][:, a:b], in_=project(t, a, b)[:])
-            nc.gpsimd.tensor_tensor(gated[t][:, a:b], plain[t][:, a:b], gate_sb[:, a:b], MULT)
+        def apply_gate(t, acc, a0, a, b):
+            nc.vector.tensor_tensor(gated[t][:, a:b], acc[:, a - a0 : b - a0], gate_sb[:, a:b], MULT)
 
-        def scatter(t, a, b):
-            listed = offsets[:, a // PER_COLUMN : b // PER_COLUMN]
-            nc.vector.tensor_copy(windows[t][:].indirect(listed), gated[t][:, a:b])
+        def place(t, a, b):
+            return windows[t][:].indirect(offsets[:, a // PER_COLUMN : b // PER_COLUMN])
+
+        def scatter_on_vector(t, a, b):
+            nc.vector.tensor_copy(place(t, a, b), gated[t][:, a:b])
+
+        def scatter_on_scalar(t, a, b):
+            nc.scalar.activation(place(t, a, b), gated[t][:, a:b], COPY)
+
+        out_rows = out_0.rearrange("(p t) c -> p t c", t=PACK)
+        pair_view = pairs[:].rearrange("p (h c e) -> p h c e", h=2, e=2)
+
+        def store_window(t):
+            nc.sync.dma_start(out=out_rows[:, t, :], in_=windows[t][:])
 
         quantize_w(0, 1)
-        a, b = PIECES[0]
-        first = project(0, a, b)
+        first = project(0, 0, FIRST)
         quantize_w(1, 2)
         quantize_w(2, PACK)
-        nc.vector.tensor_tensor(gated[0][:, a:b], first[:], gate_sb[:, a:b], MULT)
-        nc.vector.tensor_tensor(gated[1][:, a:b], project(1, a, b)[:], gate_sb[:, a:b], MULT)
-        gate_on_gpsimd(0, *PIECES[1])
-        gate_on_gpsimd(1, *PIECES[1])
-        gate_on_gpsimd(0, *PIECES[2])
-        gate_on_gpsimd(1, *PIECES[2])
-        for t in (2, 3):
-            gate_on_gpsimd(t, 0, T)
+        rest = project(0, FIRST, T)
+        acc = [None] + [project(t, 0, T) for t in range(1, PACK)]
 
-        y_grouped = keep.tile([P, U * PACK], BF16, name="y_grouped", tag="plain3", align_bytes=64)
-        out_rows = out_0.rearrange("(p t) c -> p t c", t=PACK)
-        y_view = y_grouped[:].rearrange("p (c t) -> p c t", t=PACK)
+        apply_gate(0, first, 0, 0, FIRST)
+        scatter_on_scalar(0, 0, FIRST)
+        apply_gate(0, rest, FIRST, FIRST, T)
+        scatter_on_scalar(0, FIRST, T)
+        apply_gate(1, acc[1], 0, 0, T)
+        apply_gate(2, acc[2], 0, 0, SCALAR_PART)
+        scatter_on_vector(1, 0, T)
+        scatter_on_scalar(2, 0, SCALAR_PART)
+        apply_gate(3, acc[3], 0, 0, T // 2)
+        apply_gate(3, acc[3], 0, T // 2, T)
+        apply_gate(2, acc[2], 0, SCALAR_PART, T)
+        scatter_on_scalar(3, 0, T // 2)
+        scatter_on_scalar(3, T // 2, T)
+        scatter_on_vector(2, SCALAR_PART, T)
+        for t in range(2):
+            store_window(t)
+            nc.gpsimd.tensor_scalar(pair_view[:, 0, :, t], windows[t][:], 1.0, -0.0, MULT, ADD)
+        store_window(2)
+        nc.vector.tensor_copy(out=pair_view[:, 1, :, 0], in_=windows[2][:])
+        store_window(3)
+
         chunks = [slice(a, a + CHUNK) for a in range(0, U, CHUNK)]
-        low, high = slice(0, SPLIT), slice(SPLIT, U)
+        for c in (0, 3, 1, 2):
+            nc.vector.tensor_copy(out=pair_view[:, 1, chunks[c], 1], in_=windows[3][:, chunks[c]])
 
-        def weave(t, width):
-            def source(cols):
-                return windows[t][:, cols].unsqueeze(2).to_broadcast([P, cols.stop - cols.start, width])
+        def words(dtype, cols):
+            grouped = y_grouped[:].bitcast(dtype).rearrange("p (c h) -> p c h", h=2)
+            paired = pairs[:].bitcast(dtype).rearrange("p (h c) -> p c h", h=2)
+            return grouped[:, cols], paired[:, cols]
 
-            nc.sync.dma_start(out=out_rows[:, t, :], in_=windows[t][:])
-            nc.scalar.copy(out=y_view[:, low, t : t + width], in_=source(low))
-            nc.gpsimd.tensor_scalar(y_view[:, high, t : t + width], source(high), 1.0, -0.0, MULT, ADD)
-
-        for a, b in PIECES:
-            scatter(0, a, b)
-            scatter(1, a, b)
-        weave(0, 1)
-        weave(1, 1)
-        scatter(2, 0, T)
-        weave(2, 2)
-        scatter(3, 0, T)
-        nc.sync.dma_start(out=out_rows[:, 3, :], in_=windows[3][:])
-
-        half = len(chunks) // 2
-        for mine, other in ((slice(0, CHUNK), slice(SPLIT, U - CHUNK)), (slice(CHUNK, SPLIT), slice(U - CHUNK, U))):
-            nc.vector.tensor_copy(out=y_view[:, mine, 3], in_=windows[3][:, mine])
-            nc.scalar.copy(out=y_view[:, other, 3], in_=windows[3][:, other])
+        for c in (0, 1, 2):
+            nc.scalar.copy(*words(U32, chunks[c]))
+        nc.vector.tensor_copy(*words(I32, chunks[3]))
 
         def quantize_y(cols):
             nc.vector.quantize_mx(
@@ -147,14 +158,10 @@ def tile_picked_wroute2_linnone_lo_kernel(tc, x_words, x_scales, gate, w1, dst, 
                 in_=y_grouped[:, PACK * cols.start : PACK * cols.stop],
             )
 
-        def store_words(cols):
-            words_out = out_1[0].rearrange("p n t -> p (n t)").bitcast(I32)
-            nc.sync.dma_start(out=words_out[:, cols], in_=y_codes[:, cols].bitcast(I32))
-
-        for group in ((0,256,384,),(384,512,768,),(768,1024,),):
-            for a, b in zip(group, group[1:]):
-                quantize_y(slice(a, b))
-            store_words(slice(group[0], group[-1]))
+        words_out = out_1[0].rearrange("p n t -> p (n t)").bitcast(I32)
+        for c in (0, 3, 1, 2):
+            quantize_y(chunks[c])
+            nc.sync.dma_start(out=words_out[:, chunks[c]], in_=y_codes[:, chunks[c]].bitcast(I32))
         for r in range(PACK):
             queue = nc.sync if r % 2 else nc.scalar
             queue.dma_start(out=out_2[0][r:BLOCKS:PACK, :].bitcast(I32), in_=y_scales[r:P:QUADRANT, :].bitcast(I32))

@@ -23,7 +23,8 @@ BLOCKS = 16
 PER_COLUMN = 16
 SCALAR_M = 64
 CHUNK = 256
-SCALAR_PART = 192
+SHARED = 256
+LOW = U - CHUNK
 FIRST = 128
 
 
@@ -43,9 +44,9 @@ def tile_picked_wroute2_linnone_lo_kernel(tc, x_words, x_scales, gate, w1, dst, 
         y_codes = keep.tile([P, U], U32, name="y_codes", align_bytes=64)
         y_scales = keep.tile([P, U], U8, name="y_scales", align_bytes=64)
         windows = [keep.tile([P, U], F32, name="window%d" % t) for t in range(PACK)]
-        pairs = keep.tile([P, U * PACK], BF16, name="pairs", align_bytes=64)
+        pairs = keep.tile([P, LOW * PACK], BF16, name="pairs", align_bytes=64)
         y_grouped = keep.tile([P, U * PACK], BF16, name="y_grouped", align_bytes=64)
-        gated = [keep.tile([P, T], F32, name="gated%d" % t) for t in range(PACK)]
+        gated = [keep.tile([P, T], F32, name="gated%d" % t, align_bytes=64) for t in range(PACK)]
         w_raw = [keep.tile([P, 2, N], F32, name="w_raw%d" % u) for u in range(2)]
 
         w_rows = w1.rearrange("(p j) c -> p j c", j=PACK)
@@ -61,7 +62,7 @@ def tile_picked_wroute2_linnone_lo_kernel(tc, x_words, x_scales, gate, w1, dst, 
         nc.sync.dma_start(out=gate_sb[:, T // 2 :], in_=gate[:, T // 2 :])
 
         for t in range(PACK):
-            nc.vector.memset(windows[t][:].bitcast(I32), 0)
+            (nc.gpsimd if t in (1, 2) else nc.vector).memset(windows[t][:].bitcast(I32), 0)
 
         w_view = w_grouped[:].rearrange("p (t m j) -> p m t j", t=PACK, j=PACK)
         rows_01, rows_23 = (raw[:].rearrange("p j (m t) -> p m t j", t=PACK) for raw in w_raw)
@@ -92,8 +93,8 @@ def tile_picked_wroute2_linnone_lo_kernel(tc, x_words, x_scales, gate, w1, dst, 
                 )
             return acc
 
-        def apply_gate(t, acc, a0, a, b):
-            nc.vector.tensor_tensor(gated[t][:, a:b], acc[:, a - a0 : b - a0], gate_sb[:, a:b], MULT)
+        def apply_gate(t, acc, a, b):
+            nc.vector.tensor_tensor(gated[t][:, a:b], acc[:], gate_sb[:, a:b], MULT)
 
         def place(t, a, b):
             return windows[t][:].indirect(offsets[:, a // PER_COLUMN : b // PER_COLUMN])
@@ -111,45 +112,57 @@ def tile_picked_wroute2_linnone_lo_kernel(tc, x_words, x_scales, gate, w1, dst, 
             nc.sync.dma_start(out=out_rows[:, t, :], in_=windows[t][:])
 
         quantize_w(0, 1)
-        first = project(0, 0, FIRST)
+        acc_0a = project(0, 0, FIRST)
         quantize_w(1, 2)
         quantize_w(2, PACK)
-        rest = project(0, FIRST, T)
-        acc = [None] + [project(t, 0, T) for t in range(1, PACK)]
+        acc_3a = project(3, 0, FIRST)
+        acc_1a = project(1, 0, SHARED)
+        acc_0b = project(0, FIRST, T)
+        acc_1b = project(1, SHARED, T)
+        acc_2 = project(2, 0, T)
+        acc_3b = project(3, FIRST, T)
 
-        apply_gate(0, first, 0, 0, FIRST)
+        apply_gate(0, acc_0a, 0, FIRST)
         scatter_on_scalar(0, 0, FIRST)
-        apply_gate(0, rest, FIRST, FIRST, T)
+        apply_gate(3, acc_3a, 0, FIRST)
+        scatter_on_scalar(3, 0, FIRST)
+        apply_gate(1, acc_1a, 0, SHARED)
+        apply_gate(0, acc_0b, FIRST, T)
         scatter_on_scalar(0, FIRST, T)
-        apply_gate(1, acc[1], 0, 0, T)
-        apply_gate(2, acc[2], 0, 0, SCALAR_PART)
-        scatter_on_vector(1, 0, T)
-        scatter_on_scalar(2, 0, SCALAR_PART)
-        apply_gate(3, acc[3], 0, 0, T // 2)
-        apply_gate(3, acc[3], 0, T // 2, T)
-        apply_gate(2, acc[2], 0, SCALAR_PART, T)
-        scatter_on_scalar(3, 0, T // 2)
-        scatter_on_scalar(3, T // 2, T)
-        scatter_on_vector(2, SCALAR_PART, T)
+        apply_gate(1, acc_1b, SHARED, T)
+        apply_gate(2, acc_2, 0, T)
+        scatter_on_vector(1, SHARED, T)
+        scatter_on_scalar(1, 0, SHARED)
+        apply_gate(3, acc_3b, FIRST, T)
+        scatter_on_scalar(3, FIRST, T)
+        scatter_on_vector(2, 0, T)
+        pairs_high = keep.tile([P, CHUNK * PACK], BF16, name="pairs_high", tag="gated1", align_bytes=64)
+        high_view = pairs_high[:].rearrange("p (h c e) -> p h c e", h=2, e=2)
         for t in range(2):
             store_window(t)
-            nc.gpsimd.tensor_scalar(pair_view[:, 0, :, t], windows[t][:], 1.0, -0.0, MULT, ADD)
+            nc.gpsimd.tensor_scalar(pair_view[:, 0, :, t], windows[t][:, :LOW], 1.0, -0.0, MULT, ADD)
+        for t in range(2):
+            nc.vector.tensor_copy(out=high_view[:, 0, :, t], in_=windows[t][:, LOW:])
         store_window(2)
-        nc.vector.tensor_copy(out=pair_view[:, 1, :, 0], in_=windows[2][:])
+        nc.vector.tensor_copy(out=pair_view[:, 1, :, 0], in_=windows[2][:, :LOW])
+        nc.vector.tensor_copy(out=high_view[:, 1, :, 0], in_=windows[2][:, LOW:])
         store_window(3)
 
         chunks = [slice(a, a + CHUNK) for a in range(0, U, CHUNK)]
-        for c in (0, 3, 1, 2):
+        nc.vector.tensor_copy(out=pair_view[:, 1, chunks[0], 1], in_=windows[3][:, chunks[0]])
+        nc.vector.tensor_copy(out=high_view[:, 1, :, 1], in_=windows[3][:, LOW:])
+        for c in (1, 2):
             nc.vector.tensor_copy(out=pair_view[:, 1, chunks[c], 1], in_=windows[3][:, chunks[c]])
 
-        def words(dtype, cols):
-            grouped = y_grouped[:].bitcast(dtype).rearrange("p (c h) -> p c h", h=2)
-            paired = pairs[:].bitcast(dtype).rearrange("p (h c) -> p c h", h=2)
-            return grouped[:, cols], paired[:, cols]
+        def grouped_words(dtype, cols):
+            return y_grouped[:].bitcast(dtype).rearrange("p (c h) -> p c h", h=2)[:, cols]
+
+        def paired_words(tile, dtype):
+            return tile[:].bitcast(dtype).rearrange("p (h c) -> p c h", h=2)
 
         for c in (0, 1, 2):
-            nc.scalar.copy(*words(U32, chunks[c]))
-        nc.vector.tensor_copy(*words(I32, chunks[3]))
+            nc.scalar.copy(grouped_words(U32, chunks[c]), paired_words(pairs, U32)[:, chunks[c]])
+        nc.vector.tensor_copy(grouped_words(I32, chunks[3]), paired_words(pairs_high, I32))
 
         def quantize_y(cols):
             nc.vector.quantize_mx(

@@ -21,11 +21,11 @@ PACK = 4
 QUADRANT = 32
 BLOCKS = 16
 PER_COLUMN = 16
+HALF = T // 2
+FIRST = 128
 SCALAR_M = 64
 CHUNK = 256
-SHARED = 256
 LOW = U - CHUNK
-FIRST = 128
 
 
 def tile_picked_wroute2_linnone_lo_kernel(tc, x_words, x_scales, gate, w1, dst, out_0, out_1, out_2):
@@ -44,7 +44,7 @@ def tile_picked_wroute2_linnone_lo_kernel(tc, x_words, x_scales, gate, w1, dst, 
         y_codes = keep.tile([P, U], U32, name="y_codes", align_bytes=64)
         y_scales = keep.tile([P, U], U8, name="y_scales", align_bytes=64)
         windows = [keep.tile([P, U], F32, name="window%d" % t) for t in range(PACK)]
-        pairs = keep.tile([P, LOW * PACK], BF16, name="pairs", align_bytes=64)
+        pairs_low = keep.tile([P, LOW * PACK], BF16, name="pairs_low", align_bytes=64)
         y_grouped = keep.tile([P, U * PACK], BF16, name="y_grouped", align_bytes=64)
         gated = [keep.tile([P, T], F32, name="gated%d" % t, align_bytes=64) for t in range(PACK)]
         w_raw = [keep.tile([P, 2, N], F32, name="w_raw%d" % u) for u in range(2)]
@@ -55,14 +55,15 @@ def tile_picked_wroute2_linnone_lo_kernel(tc, x_words, x_scales, gate, w1, dst, 
         for r in range(PACK):
             nc.sync.dma_start(out=x_plane[r:P:QUADRANT, :].bitcast(I32), in_=x_scales[0][r:BLOCKS:PACK, :].bitcast(I32))
         nc.sync.dma_start(out=w_raw[1][:], in_=w_rows[:, 2:4, :])
-        nc.sync.dma_start(out=x_codes[:, : T // 2].bitcast(I32), in_=x_rows[:, : T // 2])
-        nc.sync.dma_start(out=gate_sb[:, : T // 2], in_=gate[:, : T // 2])
+        nc.sync.dma_start(out=x_codes[:, :HALF].bitcast(I32), in_=x_rows[:, :HALF])
+        nc.sync.dma_start(out=gate_sb[:, :HALF], in_=gate[:, :HALF])
         nc.sync.dma_start(offsets[:], dst)
-        nc.sync.dma_start(out=x_codes[:, T // 2 :].bitcast(I32), in_=x_rows[:, T // 2 :])
-        nc.sync.dma_start(out=gate_sb[:, T // 2 :], in_=gate[:, T // 2 :])
+        nc.sync.dma_start(out=x_codes[:, HALF:].bitcast(I32), in_=x_rows[:, HALF:])
+        nc.sync.dma_start(out=gate_sb[:, HALF:], in_=gate[:, HALF:])
 
         for t in range(PACK):
-            (nc.gpsimd if t in (1, 2) else nc.vector).memset(windows[t][:].bitcast(I32), 0)
+            engine = nc.gpsimd if t in (1, 2) else nc.vector
+            engine.memset(windows[t][:].bitcast(I32), 0)
 
         w_view = w_grouped[:].rearrange("p (t m j) -> p m t j", t=PACK, j=PACK)
         rows_01, rows_23 = (raw[:].rearrange("p j (m t) -> p m t j", t=PACK) for raw in w_raw)
@@ -79,15 +80,15 @@ def tile_picked_wroute2_linnone_lo_kernel(tc, x_words, x_scales, gate, w1, dst, 
                 in_=w_grouped[:, PACK * P * t0 : PACK * P * t1],
             )
 
-        def project(t, a, b):
-            acc = psum.tile([P, b - a], F32, name="acc%d_%d" % (t, a))
-            for lo, hi in ((a, b),) if (b - a) != 384 else ((a, a + 128), (a + 128, b)):
+        def project(t, *cuts):
+            acc = psum.tile([P, cuts[-1] - cuts[0]], F32, name="acc%d_%d" % (t, cuts[0]))
+            for a, b in zip(cuts, cuts[1:]):
                 nc.tensor.matmul_mx(
-                    out=acc[:, lo - a : hi - a],
+                    out=acc[:, a - cuts[0] : b - cuts[0]],
                     lhsT=w_codes[:, P * t : P * (t + 1)].bitcast(FP8X4),
                     lhsT_scale=w_plane[:, P * t : P * (t + 1)],
-                    rhs=x_codes[:, lo:hi].bitcast(FP8X4),
-                    rhs_scale=x_plane[:, lo:hi],
+                    rhs=x_codes[:, a:b].bitcast(FP8X4),
+                    rhs_scale=x_plane[:, a:b],
                     start=True,
                     stop=True,
                 )
@@ -96,63 +97,64 @@ def tile_picked_wroute2_linnone_lo_kernel(tc, x_words, x_scales, gate, w1, dst, 
         def apply_gate(t, acc, a, b):
             nc.vector.tensor_tensor(gated[t][:, a:b], acc[:], gate_sb[:, a:b], MULT)
 
-        def place(t, a, b):
+        def places(t, a, b):
             return windows[t][:].indirect(offsets[:, a // PER_COLUMN : b // PER_COLUMN])
 
         def scatter_on_vector(t, a, b):
-            nc.vector.tensor_copy(place(t, a, b), gated[t][:, a:b])
+            nc.vector.tensor_copy(places(t, a, b), gated[t][:, a:b])
 
         def scatter_on_scalar(t, a, b):
-            nc.scalar.activation(place(t, a, b), gated[t][:, a:b], COPY)
+            nc.scalar.activation(places(t, a, b), gated[t][:, a:b], COPY)
 
+        quantize_w(0, 1)
+        acc_0_first = project(0, 0, FIRST)
+        quantize_w(1, 2)
+        quantize_w(2, PACK)
+        acc_3_first = project(3, 0, FIRST)
+        acc_1_low = project(1, 0, HALF)
+        acc_0_rest = project(0, FIRST, HALF, T)
+        acc_1_high = project(1, HALF, T)
+        acc_2 = project(2, 0, T)
+        acc_3_rest = project(3, FIRST, HALF, T)
+
+        apply_gate(0, acc_0_first, 0, FIRST)
+        scatter_on_scalar(0, 0, FIRST)
+        apply_gate(3, acc_3_first, 0, FIRST)
+        scatter_on_scalar(3, 0, FIRST)
+        apply_gate(1, acc_1_low, 0, HALF)
+        apply_gate(0, acc_0_rest, FIRST, T)
+        scatter_on_scalar(0, FIRST, T)
+        apply_gate(1, acc_1_high, HALF, T)
+        apply_gate(2, acc_2, 0, T)
+        scatter_on_vector(1, HALF, T)
+        scatter_on_scalar(1, 0, HALF)
+        apply_gate(3, acc_3_rest, FIRST, T)
+        scatter_on_scalar(3, FIRST, T)
+        scatter_on_vector(2, 0, T)
+
+        pairs_high = keep.tile([P, CHUNK * PACK], BF16, name="pairs_high", tag="gated1", align_bytes=64)
+        low_view, high_view = (tile[:].rearrange("p (h c e) -> p h c e", h=2, e=2) for tile in (pairs_low, pairs_high))
         out_rows = out_0.rearrange("(p t) c -> p t c", t=PACK)
-        pair_view = pairs[:].rearrange("p (h c e) -> p h c e", h=2, e=2)
 
         def store_window(t):
             nc.sync.dma_start(out=out_rows[:, t, :], in_=windows[t][:])
 
-        quantize_w(0, 1)
-        acc_0a = project(0, 0, FIRST)
-        quantize_w(1, 2)
-        quantize_w(2, PACK)
-        acc_3a = project(3, 0, FIRST)
-        acc_1a = project(1, 0, SHARED)
-        acc_0b = project(0, FIRST, T)
-        acc_1b = project(1, SHARED, T)
-        acc_2 = project(2, 0, T)
-        acc_3b = project(3, FIRST, T)
-
-        apply_gate(0, acc_0a, 0, FIRST)
-        scatter_on_scalar(0, 0, FIRST)
-        apply_gate(3, acc_3a, 0, FIRST)
-        scatter_on_scalar(3, 0, FIRST)
-        apply_gate(1, acc_1a, 0, SHARED)
-        apply_gate(0, acc_0b, FIRST, T)
-        scatter_on_scalar(0, FIRST, T)
-        apply_gate(1, acc_1b, SHARED, T)
-        apply_gate(2, acc_2, 0, T)
-        scatter_on_vector(1, SHARED, T)
-        scatter_on_scalar(1, 0, SHARED)
-        apply_gate(3, acc_3b, FIRST, T)
-        scatter_on_scalar(3, FIRST, T)
-        scatter_on_vector(2, 0, T)
-        pairs_high = keep.tile([P, CHUNK * PACK], BF16, name="pairs_high", tag="gated1", align_bytes=64)
-        high_view = pairs_high[:].rearrange("p (h c e) -> p h c e", h=2, e=2)
         for t in range(2):
             store_window(t)
-            nc.gpsimd.tensor_scalar(pair_view[:, 0, :, t], windows[t][:, :LOW], 1.0, -0.0, MULT, ADD)
+            nc.gpsimd.tensor_scalar(low_view[:, 0, :, t], windows[t][:, :LOW], 1.0, -0.0, MULT, ADD)
         for t in range(2):
-            nc.vector.tensor_copy(out=high_view[:, 0, :, t], in_=windows[t][:, LOW:])
+            nc.scalar.copy(out=high_view[:, 0, :, t], in_=windows[t][:, LOW:])
         store_window(2)
-        nc.vector.tensor_copy(out=pair_view[:, 1, :, 0], in_=windows[2][:, :LOW])
+        nc.vector.tensor_copy(out=low_view[:, 1, :, 0], in_=windows[2][:, :LOW])
         nc.vector.tensor_copy(out=high_view[:, 1, :, 0], in_=windows[2][:, LOW:])
         store_window(3)
 
         chunks = [slice(a, a + CHUNK) for a in range(0, U, CHUNK)]
-        nc.vector.tensor_copy(out=pair_view[:, 1, chunks[0], 1], in_=windows[3][:, chunks[0]])
-        nc.vector.tensor_copy(out=high_view[:, 1, :, 1], in_=windows[3][:, LOW:])
-        for c in (1, 2):
-            nc.vector.tensor_copy(out=pair_view[:, 1, chunks[c], 1], in_=windows[3][:, chunks[c]])
+        low_chunks, high_chunk = chunks[:-1], chunks[-1]
+        nc.vector.tensor_copy(out=low_view[:, 1, low_chunks[0], 1], in_=windows[3][:, low_chunks[0]])
+        nc.vector.tensor_copy(out=high_view[:, 1, :, 1], in_=windows[3][:, high_chunk])
+        for cols in low_chunks[1:]:
+            nc.vector.tensor_copy(out=low_view[:, 1, cols, 1], in_=windows[3][:, cols])
 
         def grouped_words(dtype, cols):
             return y_grouped[:].bitcast(dtype).rearrange("p (c h) -> p c h", h=2)[:, cols]
@@ -160,21 +162,18 @@ def tile_picked_wroute2_linnone_lo_kernel(tc, x_words, x_scales, gate, w1, dst, 
         def paired_words(tile, dtype):
             return tile[:].bitcast(dtype).rearrange("p (h c) -> p c h", h=2)
 
-        for c in (0, 1, 2):
-            nc.scalar.copy(grouped_words(U32, chunks[c]), paired_words(pairs, U32)[:, chunks[c]])
-        nc.vector.tensor_copy(grouped_words(I32, chunks[3]), paired_words(pairs_high, I32))
+        for cols in low_chunks:
+            nc.scalar.copy(grouped_words(U32, cols), paired_words(pairs_low, U32)[:, cols])
+        nc.vector.tensor_copy(grouped_words(I32, high_chunk), paired_words(pairs_high, I32))
 
-        def quantize_y(cols):
+        words_out = out_1[0].rearrange("p n t -> p (n t)").bitcast(I32)
+        for cols in [low_chunks[0], high_chunk] + low_chunks[1:]:
             nc.vector.quantize_mx(
                 out=y_codes[:, cols].bitcast(FP8X4),
                 scales=y_scales[:, cols],
                 in_=y_grouped[:, PACK * cols.start : PACK * cols.stop],
             )
-
-        words_out = out_1[0].rearrange("p n t -> p (n t)").bitcast(I32)
-        for c in (0, 3, 1, 2):
-            quantize_y(chunks[c])
-            nc.sync.dma_start(out=words_out[:, chunks[c]], in_=y_codes[:, chunks[c]].bitcast(I32))
+            nc.sync.dma_start(out=words_out[:, cols], in_=y_codes[:, cols].bitcast(I32))
         for r in range(PACK):
             queue = nc.sync if r % 2 else nc.scalar
             queue.dma_start(out=out_2[0][r:BLOCKS:PACK, :].bitcast(I32), in_=y_scales[r:P:QUADRANT, :].bitcast(I32))

@@ -22,10 +22,11 @@ QUADRANT = 32
 BLOCKS = 16
 PER_COLUMN = 16
 HALF = T // 2
+SHARED = 288
 FIRST = 128
 SCALAR_M = 64
-CHUNK = 256
-LOW = U - CHUNK
+LOW = 768
+CUTS = (LOW, 640, 256, 0)
 
 
 def tile_picked_wroute2_linnone_lo_kernel(tc, x_words, x_scales, gate, w1, dst, out_0, out_1, out_2):
@@ -70,8 +71,8 @@ def tile_picked_wroute2_linnone_lo_kernel(tc, x_words, x_scales, gate, w1, dst, 
         nc.scalar.copy(out=w_view[:, :SCALAR_M, :, 0:2], in_=rows_01[:, :SCALAR_M])
         nc.vector.tensor_copy(out=w_view[:, SCALAR_M:, :, 0:2], in_=rows_01[:, SCALAR_M:])
         nc.vector.tensor_copy(out=w_view[:, :, 0, 2:4], in_=rows_23[:, :, 0])
-        nc.scalar.copy(out=w_view[:, :, 2:4, 2:4], in_=rows_23[:, :, 2:4])
-        nc.vector.tensor_copy(out=w_view[:, :, 1, 2:4], in_=rows_23[:, :, 1])
+        nc.scalar.copy(out=w_view[:, :, 1:3, 2:4], in_=rows_23[:, :, 1:3])
+        nc.vector.tensor_copy(out=w_view[:, :, 3, 2:4], in_=rows_23[:, :, 3])
 
         def quantize_w(t0, t1):
             nc.vector.quantize_mx(
@@ -95,7 +96,7 @@ def tile_picked_wroute2_linnone_lo_kernel(tc, x_words, x_scales, gate, w1, dst, 
             return acc
 
         def apply_gate(t, acc, a, b):
-            nc.vector.tensor_tensor(gated[t][:, a:b], acc[:], gate_sb[:, a:b], MULT)
+            nc.vector.tensor_tensor(gated[t][:, a:b], acc, gate_sb[:, a:b], MULT)
 
         def places(t, a, b):
             return windows[t][:].indirect(offsets[:, a // PER_COLUMN : b // PER_COLUMN])
@@ -108,31 +109,30 @@ def tile_picked_wroute2_linnone_lo_kernel(tc, x_words, x_scales, gate, w1, dst, 
 
         quantize_w(0, 1)
         acc_0_first = project(0, 0, FIRST)
-        quantize_w(1, 2)
-        quantize_w(2, PACK)
+        quantize_w(3, PACK)
+        quantize_w(1, 3)
         acc_3_first = project(3, 0, FIRST)
-        acc_1_low = project(1, 0, HALF)
         acc_0_rest = project(0, FIRST, HALF, T)
-        acc_1_high = project(1, HALF, T)
+        acc_1 = project(1, 0, T)
         acc_2 = project(2, 0, T)
         acc_3_rest = project(3, FIRST, HALF, T)
 
-        apply_gate(0, acc_0_first, 0, FIRST)
+        apply_gate(0, acc_0_first[:], 0, FIRST)
         scatter_on_scalar(0, 0, FIRST)
-        apply_gate(3, acc_3_first, 0, FIRST)
+        apply_gate(3, acc_3_first[:], 0, FIRST)
         scatter_on_scalar(3, 0, FIRST)
-        apply_gate(1, acc_1_low, 0, HALF)
-        apply_gate(0, acc_0_rest, FIRST, T)
+        apply_gate(0, acc_0_rest[:], FIRST, T)
         scatter_on_scalar(0, FIRST, T)
-        apply_gate(1, acc_1_high, HALF, T)
-        apply_gate(2, acc_2, 0, T)
-        scatter_on_vector(1, HALF, T)
-        scatter_on_scalar(1, 0, HALF)
-        apply_gate(3, acc_3_rest, FIRST, T)
+        apply_gate(1, acc_1[:, :SHARED], 0, SHARED)
+        apply_gate(1, acc_1[:, SHARED:], SHARED, T)
+        scatter_on_vector(1, 0, SHARED)
+        scatter_on_scalar(1, SHARED, T)
+        apply_gate(2, acc_2[:], 0, T)
+        apply_gate(3, acc_3_rest[:], FIRST, T)
         scatter_on_scalar(3, FIRST, T)
         scatter_on_vector(2, 0, T)
 
-        pairs_high = keep.tile([P, CHUNK * PACK], BF16, name="pairs_high", tag="gated1", align_bytes=64)
+        pairs_high = keep.tile([P, (U - LOW) * PACK], BF16, name="pairs_high", tag="gated1", align_bytes=64)
         low_view, high_view = (tile[:].rearrange("p (h c e) -> p h c e", h=2, e=2) for tile in (pairs_low, pairs_high))
         out_rows = out_0.rearrange("(p t) c -> p t c", t=PACK)
 
@@ -149,12 +149,12 @@ def tile_picked_wroute2_linnone_lo_kernel(tc, x_words, x_scales, gate, w1, dst, 
         nc.vector.tensor_copy(out=high_view[:, 1, :, 0], in_=windows[2][:, LOW:])
         store_window(3)
 
-        chunks = [slice(a, a + CHUNK) for a in range(0, U, CHUNK)]
-        low_chunks, high_chunk = chunks[:-1], chunks[-1]
-        nc.vector.tensor_copy(out=low_view[:, 1, low_chunks[0], 1], in_=windows[3][:, low_chunks[0]])
-        nc.vector.tensor_copy(out=high_view[:, 1, :, 1], in_=windows[3][:, high_chunk])
-        for cols in low_chunks[1:]:
+        short, middle, last = (slice(a, b) for a, b in zip(CUTS[1:], CUTS))
+        high = slice(LOW, U)
+        for cols in (short, middle):
             nc.vector.tensor_copy(out=low_view[:, 1, cols, 1], in_=windows[3][:, cols])
+        nc.vector.tensor_copy(out=high_view[:, 1, :, 1], in_=windows[3][:, high])
+        nc.vector.tensor_copy(out=low_view[:, 1, last, 1], in_=windows[3][:, last])
 
         def grouped_words(dtype, cols):
             return y_grouped[:].bitcast(dtype).rearrange("p (c h) -> p c h", h=2)[:, cols]
@@ -162,18 +162,20 @@ def tile_picked_wroute2_linnone_lo_kernel(tc, x_words, x_scales, gate, w1, dst, 
         def paired_words(tile, dtype):
             return tile[:].bitcast(dtype).rearrange("p (h c) -> p c h", h=2)
 
-        for cols in low_chunks:
+        for cols in (short, middle, last):
             nc.scalar.copy(grouped_words(U32, cols), paired_words(pairs_low, U32)[:, cols])
-        nc.vector.tensor_copy(grouped_words(I32, high_chunk), paired_words(pairs_high, I32))
+        nc.vector.tensor_copy(grouped_words(I32, high), paired_words(pairs_high, I32))
 
         words_out = out_1[0].rearrange("p n t -> p (n t)").bitcast(I32)
-        for cols in [low_chunks[0], high_chunk] + low_chunks[1:]:
-            nc.vector.quantize_mx(
-                out=y_codes[:, cols].bitcast(FP8X4),
-                scales=y_scales[:, cols],
-                in_=y_grouped[:, PACK * cols.start : PACK * cols.stop],
-            )
-            nc.sync.dma_start(out=words_out[:, cols], in_=y_codes[:, cols].bitcast(I32))
+        for group in ((short, high), (middle,), (last,)):
+            for cols in group:
+                nc.vector.quantize_mx(
+                    out=y_codes[:, cols].bitcast(FP8X4),
+                    scales=y_scales[:, cols],
+                    in_=y_grouped[:, PACK * cols.start : PACK * cols.stop],
+                )
+            stored = slice(group[0].start, group[-1].stop)
+            nc.sync.dma_start(out=words_out[:, stored], in_=y_codes[:, stored].bitcast(I32))
         for r in range(PACK):
             queue = nc.sync if r % 2 else nc.scalar
             queue.dma_start(out=out_2[0][r:BLOCKS:PACK, :].bitcast(I32), in_=y_scales[r:P:QUADRANT, :].bitcast(I32))

@@ -22,11 +22,11 @@ QUADRANT = 32
 BLOCKS = 16
 PER_COLUMN = 16
 HALF = T // 2
-SHARED = 288
+SHARED = 320
 FIRST = 128
 SCALAR_M = 64
 LOW = 768
-CUTS = (LOW, 640, 256, 0)
+PIECE = 256
 
 
 def tile_picked_wroute2_linnone_lo_kernel(tc, x_words, x_scales, gate, w1, dst, out_0, out_1, out_2):
@@ -45,7 +45,7 @@ def tile_picked_wroute2_linnone_lo_kernel(tc, x_words, x_scales, gate, w1, dst, 
         y_codes = keep.tile([P, U], U32, name="y_codes", align_bytes=64)
         y_scales = keep.tile([P, U], U8, name="y_scales", align_bytes=64)
         windows = [keep.tile([P, U], F32, name="window%d" % t) for t in range(PACK)]
-        pairs_low = keep.tile([P, LOW * PACK], BF16, name="pairs_low", align_bytes=64)
+        pairs = keep.tile([P, U * PACK], BF16, name="pairs", align_bytes=64)
         y_grouped = keep.tile([P, U * PACK], BF16, name="y_grouped", align_bytes=64)
         gated = [keep.tile([P, T], F32, name="gated%d" % t, align_bytes=64) for t in range(PACK)]
         w_raw = [keep.tile([P, 2, N], F32, name="w_raw%d" % u) for u in range(2)]
@@ -132,8 +132,7 @@ def tile_picked_wroute2_linnone_lo_kernel(tc, x_words, x_scales, gate, w1, dst, 
         scatter_on_scalar(3, FIRST, T)
         scatter_on_vector(2, 0, T)
 
-        pairs_high = keep.tile([P, (U - LOW) * PACK], BF16, name="pairs_high", tag="gated1", align_bytes=64)
-        low_view, high_view = (tile[:].rearrange("p (h c e) -> p h c e", h=2, e=2) for tile in (pairs_low, pairs_high))
+        pair_view = pairs[:].rearrange("p (h c e) -> p h c e", h=2, e=2)
         out_rows = out_0.rearrange("(p t) c -> p t c", t=PACK)
 
         def store_window(t):
@@ -141,40 +140,38 @@ def tile_picked_wroute2_linnone_lo_kernel(tc, x_words, x_scales, gate, w1, dst, 
 
         for t in range(2):
             store_window(t)
-            nc.gpsimd.tensor_scalar(low_view[:, 0, :, t], windows[t][:, :LOW], 1.0, -0.0, MULT, ADD)
-        for t in range(2):
-            nc.scalar.copy(out=high_view[:, 0, :, t], in_=windows[t][:, LOW:])
+            nc.gpsimd.tensor_scalar(pair_view[:, 0, :, t], windows[t][:], 1.0, -0.0, MULT, ADD)
         store_window(2)
-        nc.vector.tensor_copy(out=low_view[:, 1, :, 0], in_=windows[2][:, :LOW])
-        nc.vector.tensor_copy(out=high_view[:, 1, :, 0], in_=windows[2][:, LOW:])
         store_window(3)
-
-        short, middle, last = (slice(a, b) for a, b in zip(CUTS[1:], CUTS))
-        high = slice(LOW, U)
-        for cols in (short, middle):
-            nc.vector.tensor_copy(out=low_view[:, 1, cols, 1], in_=windows[3][:, cols])
-        nc.vector.tensor_copy(out=high_view[:, 1, :, 1], in_=windows[3][:, high])
-        nc.vector.tensor_copy(out=low_view[:, 1, last, 1], in_=windows[3][:, last])
+        first, second, third, high = (slice(a, a + PIECE) for a in range(0, U, PIECE))
+        halves = [slice(a, a + PIECE // 2) for a in range(0, U, PIECE // 2)]
+        nc.scalar.copy(out=pair_view[:, 1, high, 0], in_=windows[2][:, high])
+        for cols in halves[-2:]:
+            nc.scalar.copy(out=pair_view[:, 1, cols, 1], in_=windows[3][:, cols])
+        nc.vector.tensor_copy(out=pair_view[:, 1, :LOW, 0], in_=windows[2][:, :LOW])
+        for cols in (third, second, first):
+            nc.vector.tensor_copy(out=pair_view[:, 1, cols, 1], in_=windows[3][:, cols])
 
         def grouped_words(dtype, cols):
             return y_grouped[:].bitcast(dtype).rearrange("p (c h) -> p c h", h=2)[:, cols]
 
-        def paired_words(tile, dtype):
-            return tile[:].bitcast(dtype).rearrange("p (h c) -> p c h", h=2)
+        def paired_words(dtype, cols):
+            return pairs[:].bitcast(dtype).rearrange("p (h c) -> p c h", h=2)[:, cols]
 
-        for cols in (short, middle, last):
-            nc.scalar.copy(grouped_words(U32, cols), paired_words(pairs_low, U32)[:, cols])
-        nc.vector.tensor_copy(grouped_words(I32, high), paired_words(pairs_high, I32))
+        for cols in (third, halves[0]):
+            nc.vector.tensor_copy(grouped_words(I32, cols), paired_words(I32, cols))
+        for cols in (halves[-2], halves[-1], second, halves[1]):
+            nc.scalar.copy(grouped_words(U32, cols), paired_words(U32, cols))
 
         words_out = out_1[0].rearrange("p n t -> p (n t)").bitcast(I32)
-        for group in ((short, high), (middle,), (last,)):
+        for group in ((high, third), (second,), (first,)):
             for cols in group:
                 nc.vector.quantize_mx(
                     out=y_codes[:, cols].bitcast(FP8X4),
                     scales=y_scales[:, cols],
                     in_=y_grouped[:, PACK * cols.start : PACK * cols.stop],
                 )
-            stored = slice(group[0].start, group[-1].stop)
+            stored = slice(group[-1].start, group[0].stop)
             nc.sync.dma_start(out=words_out[:, stored], in_=y_codes[:, stored].bitcast(I32))
         for r in range(PACK):
             queue = nc.sync if r % 2 else nc.scalar

@@ -22,7 +22,7 @@ QUADRANT = 32
 BLOCKS = 16
 PER_COLUMN = 16
 HALF = T // 2
-SHARED = 320
+SHARED = 288
 FIRST = 128
 SCALAR_M = 64
 LOW = 768

@@ -25,7 +25,7 @@ HALF = T // 2
 SHARED = 288
 FIRST = 128
 SCALAR_M = 64
-LOW = 768
+LOW = 896
 PIECE = 256
 
 
@@ -45,7 +45,7 @@ def tile_picked_wroute2_linnone_lo_kernel(tc, x_words, x_scales, gate, w1, dst, 
         y_codes = keep.tile([P, U], U32, name="y_codes", align_bytes=64)
         y_scales = keep.tile([P, U], U8, name="y_scales", align_bytes=64)
         windows = [keep.tile([P, U], F32, name="window%d" % t) for t in range(PACK)]
-        pairs = keep.tile([P, U * PACK], BF16, name="pairs", align_bytes=64)
+        pairs = keep.tile([P, LOW * PACK], BF16, name="pairs", align_bytes=64)
         y_grouped = keep.tile([P, U * PACK], BF16, name="y_grouped", align_bytes=64)
         gated = [keep.tile([P, T], F32, name="gated%d" % t, align_bytes=64) for t in range(PACK)]
         w_raw = [keep.tile([P, 2, N], F32, name="w_raw%d" % u) for u in range(2)]
@@ -132,7 +132,8 @@ def tile_picked_wroute2_linnone_lo_kernel(tc, x_words, x_scales, gate, w1, dst, 
         scatter_on_scalar(3, FIRST, T)
         scatter_on_vector(2, 0, T)
 
-        pair_view = pairs[:].rearrange("p (h c e) -> p h c e", h=2, e=2)
+        pairs_high = keep.tile([P, (U - LOW) * PACK], BF16, name="pairs_high", tag="gated1", align_bytes=64)
+        pair_view, high_view = (tile[:].rearrange("p (h c e) -> p h c e", h=2, e=2) for tile in (pairs, pairs_high))
         out_rows = out_0.rearrange("(p t) c -> p t c", t=PACK)
 
         def store_window(t):
@@ -140,16 +141,15 @@ def tile_picked_wroute2_linnone_lo_kernel(tc, x_words, x_scales, gate, w1, dst, 
 
         for t in range(2):
             store_window(t)
-            nc.gpsimd.tensor_scalar(pair_view[:, 0, :, t], windows[t][:], 1.0, -0.0, MULT, ADD)
+            nc.gpsimd.tensor_scalar(pair_view[:, 0, :, t], windows[t][:, :LOW], 1.0, -0.0, MULT, ADD)
         store_window(2)
         store_window(3)
         first, second, third, high = (slice(a, a + PIECE) for a in range(0, U, PIECE))
         halves = [slice(a, a + PIECE // 2) for a in range(0, U, PIECE // 2)]
-        nc.scalar.copy(out=pair_view[:, 1, high, 0], in_=windows[2][:, high])
-        for cols in halves[-2:]:
-            nc.scalar.copy(out=pair_view[:, 1, cols, 1], in_=windows[3][:, cols])
+        for t in range(PACK):
+            nc.scalar.copy(out=high_view[:, t // 2, :, t % 2], in_=windows[t][:, LOW:])
         nc.vector.tensor_copy(out=pair_view[:, 1, :LOW, 0], in_=windows[2][:, :LOW])
-        for cols in (third, second, first):
+        for cols in (halves[-2], third, second, first):
             nc.vector.tensor_copy(out=pair_view[:, 1, cols, 1], in_=windows[3][:, cols])
 
         def grouped_words(dtype, cols):
@@ -160,7 +160,9 @@ def tile_picked_wroute2_linnone_lo_kernel(tc, x_words, x_scales, gate, w1, dst, 
 
         for cols in (third, halves[0]):
             nc.vector.tensor_copy(grouped_words(I32, cols), paired_words(I32, cols))
-        for cols in (halves[-2], halves[-1], second, halves[1]):
+        nc.scalar.copy(grouped_words(U32, halves[-2]), paired_words(U32, halves[-2]))
+        nc.scalar.copy(grouped_words(U32, halves[-1]), pairs_high[:].bitcast(U32).rearrange("p (h c) -> p c h", h=2))
+        for cols in (second, halves[1]):
             nc.scalar.copy(grouped_words(U32, cols), paired_words(U32, cols))
 
         words_out = out_1[0].rearrange("p n t -> p (n t)").bitcast(I32)

@@ -22,11 +22,11 @@ QUADRANT = 32
 BLOCKS = 16
 PER_COLUMN = 16
 HALF = T // 2
-SHARED = 288
+SHARED = 160
 FIRST = 128
 SCALAR_M = 64
-LOW = 896
 PIECE = 256
+ALIGN = 256
 
 
 def tile_picked_wroute2_linnone_lo_kernel(tc, x_words, x_scales, gate, w1, dst, out_0, out_1, out_2):
@@ -36,43 +36,43 @@ def tile_picked_wroute2_linnone_lo_kernel(tc, x_words, x_scales, gate, w1, dst, 
         psum = ctx.enter_context(tc.psum_pool(name="psum", bufs=1))
 
         offsets = keep.tile([P, T // PER_COLUMN], U16, name="offsets")
-        x_codes = keep.tile([P, T], U32, name="x_codes", align_bytes=64)
-        x_plane = keep.tile([P, T], U8, name="x_plane", align_bytes=64)
-        w_plane = keep.tile([P, N], U8, name="w_plane", align_bytes=64)
-        gate_sb = keep.tile([P, T], F32, name="gate_sb")
-        w_grouped = keep.tile([P, N * PACK], BF16, name="w_grouped", align_bytes=64)
-        w_codes = keep.tile([P, N], U32, name="w_codes", align_bytes=64)
-        y_codes = keep.tile([P, U], U32, name="y_codes", align_bytes=64)
-        y_scales = keep.tile([P, U], U8, name="y_scales", align_bytes=64)
-        windows = [keep.tile([P, U], F32, name="window%d" % t) for t in range(PACK)]
-        pairs = keep.tile([P, LOW * PACK], BF16, name="pairs", align_bytes=64)
-        y_grouped = keep.tile([P, U * PACK], BF16, name="y_grouped", align_bytes=64)
-        gated = [keep.tile([P, T], F32, name="gated%d" % t, align_bytes=64) for t in range(PACK)]
-        w_raw = [keep.tile([P, 2, N], F32, name="w_raw%d" % u) for u in range(2)]
+        x_codes = keep.tile([P, T], U32, name="x_codes", align_bytes=ALIGN)
+        x_plane = keep.tile([P, T], U8, name="x_plane", align_bytes=ALIGN)
+        w_plane = keep.tile([P, N], U8, name="w_plane", align_bytes=ALIGN)
+        gate_sb = keep.tile([P, T], F32, name="gate_sb", align_bytes=ALIGN)
+        ones = keep.tile([P, 1], F32, name="ones")
+        w_grouped = keep.tile([P, N * PACK], BF16, name="w_grouped", align_bytes=ALIGN)
+        w_codes = keep.tile([P, N], U32, name="w_codes", align_bytes=ALIGN)
+        y_codes = keep.tile([P, U], U32, name="y_codes", align_bytes=ALIGN)
+        y_scales = keep.tile([P, U], U8, name="y_scales", align_bytes=ALIGN)
+        windows = {t: keep.tile([P, U], F32, name="window%d" % t, align_bytes=ALIGN) for t in (0, 1)}
+        pairs = keep.tile([P, U * PACK], BF16, name="pairs", align_bytes=ALIGN)
+        y_grouped = keep.tile([P, U * PACK], BF16, name="y_grouped", align_bytes=ALIGN)
+        gated = [keep.tile([P, T], F32, name="gated%d" % t, align_bytes=ALIGN) for t in range(PACK)]
+        w_raw = [keep.tile([P, 2, N], F32, name="w_raw%d" % u, align_bytes=ALIGN) for u in range(2)]
 
         w_rows = w1.rearrange("(p j) c -> p j c", j=PACK)
         x_rows = x_words[0].rearrange("p n t -> p (n t)").bitcast(I32)
         nc.sync.dma_start(out=w_raw[0][:], in_=w_rows[:, 0:2, :])
+        nc.sync.dma_start(out=w_raw[1][:], in_=w_rows[:, 2:4, :])
+        nc.sync.dma_start(out=x_codes[:].bitcast(I32), in_=x_rows)
         for r in range(PACK):
             nc.sync.dma_start(out=x_plane[r:P:QUADRANT, :].bitcast(I32), in_=x_scales[0][r:BLOCKS:PACK, :].bitcast(I32))
-        nc.sync.dma_start(out=w_raw[1][:], in_=w_rows[:, 2:4, :])
-        nc.sync.dma_start(out=x_codes[:, :HALF].bitcast(I32), in_=x_rows[:, :HALF])
         nc.sync.dma_start(out=gate_sb[:, :HALF], in_=gate[:, :HALF])
-        nc.sync.dma_start(offsets[:], dst)
-        nc.sync.dma_start(out=x_codes[:, HALF:].bitcast(I32), in_=x_rows[:, HALF:])
         nc.sync.dma_start(out=gate_sb[:, HALF:], in_=gate[:, HALF:])
+        nc.sync.dma_start(offsets[:], dst)
 
-        for t in range(PACK):
-            engine = nc.gpsimd if t in (1, 2) else nc.vector
-            engine.memset(windows[t][:].bitcast(I32), 0)
+        for t in (0, 1):
+            nc.vector.memset(windows[t][:].bitcast(I32), 0)
+        nc.vector.memset(ones[:], 1.0)
 
         w_view = w_grouped[:].rearrange("p (t m j) -> p m t j", t=PACK, j=PACK)
         rows_01, rows_23 = (raw[:].rearrange("p j (m t) -> p m t j", t=PACK) for raw in w_raw)
         nc.scalar.copy(out=w_view[:, :SCALAR_M, :, 0:2], in_=rows_01[:, :SCALAR_M])
         nc.vector.tensor_copy(out=w_view[:, SCALAR_M:, :, 0:2], in_=rows_01[:, SCALAR_M:])
         nc.vector.tensor_copy(out=w_view[:, :, 0, 2:4], in_=rows_23[:, :, 0])
-        nc.scalar.copy(out=w_view[:, :, 1:3, 2:4], in_=rows_23[:, :, 1:3])
-        nc.vector.tensor_copy(out=w_view[:, :, 3, 2:4], in_=rows_23[:, :, 3])
+        nc.scalar.copy(out=w_view[:, :, 2:4, 2:4], in_=rows_23[:, :, 2:4])
+        nc.vector.tensor_copy(out=w_view[:, :, 1, 2:4], in_=rows_23[:, :, 1])
 
         def quantize_w(t0, t1):
             nc.vector.quantize_mx(
@@ -109,31 +109,30 @@ def tile_picked_wroute2_linnone_lo_kernel(tc, x_words, x_scales, gate, w1, dst, 
 
         quantize_w(0, 1)
         acc_0_first = project(0, 0, FIRST)
-        quantize_w(3, PACK)
-        quantize_w(1, 3)
-        acc_3_first = project(3, 0, FIRST)
+        quantize_w(1, 2)
+        quantize_w(2, PACK)
         acc_0_rest = project(0, FIRST, HALF, T)
         acc_1 = project(1, 0, T)
         acc_2 = project(2, 0, T)
-        acc_3_rest = project(3, FIRST, HALF, T)
+        acc_3 = project(3, 0, T)
+
+        for t, tag in ((2, "w_grouped"), (3, "w_codes")):
+            windows.setdefault(t, keep.tile([P, U], F32, name="window%d" % t, tag=tag, align_bytes=ALIGN))
+            nc.gpsimd.memset(windows[t][:].bitcast(I32), 0)
 
         apply_gate(0, acc_0_first[:], 0, FIRST)
         scatter_on_scalar(0, 0, FIRST)
-        apply_gate(3, acc_3_first[:], 0, FIRST)
-        scatter_on_scalar(3, 0, FIRST)
         apply_gate(0, acc_0_rest[:], FIRST, T)
         scatter_on_scalar(0, FIRST, T)
-        apply_gate(1, acc_1[:, :SHARED], 0, SHARED)
-        apply_gate(1, acc_1[:, SHARED:], SHARED, T)
-        scatter_on_vector(1, 0, SHARED)
-        scatter_on_scalar(1, SHARED, T)
+        apply_gate(1, acc_1[:], 0, T)
         apply_gate(2, acc_2[:], 0, T)
-        apply_gate(3, acc_3_rest[:], FIRST, T)
-        scatter_on_scalar(3, FIRST, T)
-        scatter_on_vector(2, 0, T)
+        apply_gate(3, acc_3[:], 0, T)
+        scatter_on_vector(1, 0, T)
+        scatter_on_scalar(2, 0, SHARED)
+        nc.scalar.activation(places(3, 0, T), gated[3][:], COPY, scale=ones[:])
+        scatter_on_vector(2, SHARED, T)
 
-        pairs_high = keep.tile([P, (U - LOW) * PACK], BF16, name="pairs_high", tag="gated1", align_bytes=64)
-        pair_view, high_view = (tile[:].rearrange("p (h c e) -> p h c e", h=2, e=2) for tile in (pairs, pairs_high))
+        pair_view = pairs[:].rearrange("p (h c e) -> p h c e", h=2, e=2)
         out_rows = out_0.rearrange("(p t) c -> p t c", t=PACK)
 
         def store_window(t):
@@ -141,15 +140,16 @@ def tile_picked_wroute2_linnone_lo_kernel(tc, x_words, x_scales, gate, w1, dst, 
 
         for t in range(2):
             store_window(t)
-            nc.gpsimd.tensor_scalar(pair_view[:, 0, :, t], windows[t][:, :LOW], 1.0, -0.0, MULT, ADD)
+            nc.gpsimd.tensor_scalar(pair_view[:, 0, :, t], windows[t][:], 1.0, -0.0, MULT, ADD)
         store_window(2)
         store_window(3)
         first, second, third, high = (slice(a, a + PIECE) for a in range(0, U, PIECE))
         halves = [slice(a, a + PIECE // 2) for a in range(0, U, PIECE // 2)]
-        for t in range(PACK):
-            nc.scalar.copy(out=high_view[:, t // 2, :, t % 2], in_=windows[t][:, LOW:])
-        nc.vector.tensor_copy(out=pair_view[:, 1, :LOW, 0], in_=windows[2][:, :LOW])
-        for cols in (halves[-2], third, second, first):
+        nc.scalar.copy(out=pair_view[:, 1, high, 0], in_=windows[2][:, high])
+        for cols in halves[-2:]:
+            nc.scalar.copy(out=pair_view[:, 1, cols, 1], in_=windows[3][:, cols])
+        nc.vector.tensor_copy(out=pair_view[:, 1, : high.start, 0], in_=windows[2][:, : high.start])
+        for cols in (third, second, first):
             nc.vector.tensor_copy(out=pair_view[:, 1, cols, 1], in_=windows[3][:, cols])
 
         def grouped_words(dtype, cols):
@@ -160,9 +160,7 @@ def tile_picked_wroute2_linnone_lo_kernel(tc, x_words, x_scales, gate, w1, dst, 
 
         for cols in (third, halves[0]):
             nc.vector.tensor_copy(grouped_words(I32, cols), paired_words(I32, cols))
-        nc.scalar.copy(grouped_words(U32, halves[-2]), paired_words(U32, halves[-2]))
-        nc.scalar.copy(grouped_words(U32, halves[-1]), pairs_high[:].bitcast(U32).rearrange("p (h c) -> p c h", h=2))
-        for cols in (second, halves[1]):
+        for cols in (halves[-2], halves[-1], second, halves[1]):
             nc.scalar.copy(grouped_words(U32, cols), paired_words(U32, cols))
 
         words_out = out_1[0].rearrange("p n t -> p (n t)").bitcast(I32)

@@ -22,9 +22,10 @@ QUADRANT = 32
 BLOCKS = 16
 PER_COLUMN = 16
 HALF = T // 2
-SHARED = 160
+SHARED = 192
 FIRST = 128
 SCALAR_M = 64
+LATE_M = 96
 PIECE = 256
 ALIGN = 256
 
@@ -37,14 +38,14 @@ def tile_picked_wroute2_linnone_lo_kernel(tc, x_words, x_scales, gate, w1, dst, 
 
         offsets = keep.tile([P, T // PER_COLUMN], U16, name="offsets")
         x_codes = keep.tile([P, T], U32, name="x_codes", align_bytes=ALIGN)
-        x_plane = keep.tile([P, T], U8, name="x_plane", align_bytes=ALIGN)
+        x_plane = keep.tile([P, HALF], U8, name="x_plane", align_bytes=ALIGN)
         w_plane = keep.tile([P, N], U8, name="w_plane", align_bytes=ALIGN)
         gate_sb = keep.tile([P, T], F32, name="gate_sb", align_bytes=ALIGN)
         ones = keep.tile([P, 1], F32, name="ones")
         w_grouped = keep.tile([P, N * PACK], BF16, name="w_grouped", align_bytes=ALIGN)
         w_codes = keep.tile([P, N], U32, name="w_codes", align_bytes=ALIGN)
         y_codes = keep.tile([P, U], U32, name="y_codes", align_bytes=ALIGN)
-        y_scales = keep.tile([P, U], U8, name="y_scales", align_bytes=ALIGN)
+        y_scales = keep.tile([P, U // 2], U8, name="y_scales", align_bytes=ALIGN)
         windows = {t: keep.tile([P, U], F32, name="window%d" % t, align_bytes=ALIGN) for t in (0, 1)}
         pairs = keep.tile([P, U * PACK], BF16, name="pairs", align_bytes=ALIGN)
         y_grouped = keep.tile([P, U * PACK], BF16, name="y_grouped", align_bytes=ALIGN)
@@ -54,13 +55,15 @@ def tile_picked_wroute2_linnone_lo_kernel(tc, x_words, x_scales, gate, w1, dst, 
         w_rows = w1.rearrange("(p j) c -> p j c", j=PACK)
         x_rows = x_words[0].rearrange("p n t -> p (n t)").bitcast(I32)
         nc.sync.dma_start(out=w_raw[0][:], in_=w_rows[:, 0:2, :])
+        x_scale_rows = x_scales[0].bitcast(I32).rearrange("(q r) (a c) -> q a r c", r=PACK, a=2)
+        for q in range(PACK):
+            nc.sync.dma_start(out=x_plane[QUADRANT * q : QUADRANT * q + 2 * PACK, :].bitcast(I32), in_=x_scale_rows[q])
         nc.sync.dma_start(out=w_raw[1][:], in_=w_rows[:, 2:4, :])
-        nc.sync.dma_start(out=x_codes[:].bitcast(I32), in_=x_rows)
-        for r in range(PACK):
-            nc.sync.dma_start(out=x_plane[r:P:QUADRANT, :].bitcast(I32), in_=x_scales[0][r:BLOCKS:PACK, :].bitcast(I32))
+        nc.sync.dma_start(out=x_codes[:, :HALF].bitcast(I32), in_=x_rows[:, :HALF])
         nc.sync.dma_start(out=gate_sb[:, :HALF], in_=gate[:, :HALF])
-        nc.sync.dma_start(out=gate_sb[:, HALF:], in_=gate[:, HALF:])
         nc.sync.dma_start(offsets[:], dst)
+        nc.sync.dma_start(out=x_codes[:, HALF:].bitcast(I32), in_=x_rows[:, HALF:])
+        nc.sync.dma_start(out=gate_sb[:, HALF:], in_=gate[:, HALF:])
 
         for t in (0, 1):
             nc.vector.memset(windows[t][:].bitcast(I32), 0)
@@ -70,8 +73,9 @@ def tile_picked_wroute2_linnone_lo_kernel(tc, x_words, x_scales, gate, w1, dst, 
         rows_01, rows_23 = (raw[:].rearrange("p j (m t) -> p m t j", t=PACK) for raw in w_raw)
         nc.scalar.copy(out=w_view[:, :SCALAR_M, :, 0:2], in_=rows_01[:, :SCALAR_M])
         nc.vector.tensor_copy(out=w_view[:, SCALAR_M:, :, 0:2], in_=rows_01[:, SCALAR_M:])
-        nc.vector.tensor_copy(out=w_view[:, :, 0, 2:4], in_=rows_23[:, :, 0])
-        nc.scalar.copy(out=w_view[:, :, 2:4, 2:4], in_=rows_23[:, :, 2:4])
+        nc.vector.tensor_copy(out=w_view[:, :LATE_M, 0, 2:4], in_=rows_23[:, :LATE_M, 0])
+        nc.scalar.copy(out=w_view[:, LATE_M:, 0, 2:4], in_=rows_23[:, LATE_M:, 0])
+        nc.scalar.copy(out=w_view[:, :LATE_M, 2:4, 2:4], in_=rows_23[:, :LATE_M, 2:4])
         nc.vector.tensor_copy(out=w_view[:, :, 1, 2:4], in_=rows_23[:, :, 1])
 
         def quantize_w(t0, t1):
@@ -81,15 +85,16 @@ def tile_picked_wroute2_linnone_lo_kernel(tc, x_words, x_scales, gate, w1, dst, 
                 in_=w_grouped[:, PACK * P * t0 : PACK * P * t1],
             )
 
-        def project(t, *cuts):
-            acc = psum.tile([P, cuts[-1] - cuts[0]], F32, name="acc%d_%d" % (t, cuts[0]))
-            for a, b in zip(cuts, cuts[1:]):
+        def project(t, *spans):
+            base = min(a for a, b in spans)
+            acc = psum.tile([P, max(b for a, b in spans) - base], F32, name="acc%d_%d" % (t, base))
+            for a, b in spans:
                 nc.tensor.matmul_mx(
-                    out=acc[:, a - cuts[0] : b - cuts[0]],
+                    out=acc[:, a - base : b - base],
                     lhsT=w_codes[:, P * t : P * (t + 1)].bitcast(FP8X4),
                     lhsT_scale=w_plane[:, P * t : P * (t + 1)],
                     rhs=x_codes[:, a:b].bitcast(FP8X4),
-                    rhs_scale=x_plane[:, a:b],
+                    rhs_scale=x_plane[PACK * (a // HALF) :, a % HALF : a % HALF + b - a],
                     start=True,
                     stop=True,
                 )
@@ -108,13 +113,15 @@ def tile_picked_wroute2_linnone_lo_kernel(tc, x_words, x_scales, gate, w1, dst, 
             nc.scalar.activation(places(t, a, b), gated[t][:, a:b], COPY)
 
         quantize_w(0, 1)
-        acc_0_first = project(0, 0, FIRST)
+        acc_0_first = project(0, (0, FIRST))
         quantize_w(1, 2)
+        nc.vector.tensor_copy(out=w_view[:, LATE_M:, 2:4, 2:4], in_=rows_23[:, LATE_M:, 2:4])
         quantize_w(2, PACK)
-        acc_0_rest = project(0, FIRST, HALF, T)
-        acc_1 = project(1, 0, T)
-        acc_2 = project(2, 0, T)
-        acc_3 = project(3, 0, T)
+        acc_0_rest = project(0, (FIRST, HALF), (HALF, T))
+        acc_1_high = project(1, (HALF, T))
+        acc_1_low = project(1, (0, HALF))
+        acc_2 = project(2, (HALF, T), (0, HALF))
+        acc_3 = project(3, (HALF, T), (0, HALF))
 
         for t, tag in ((2, "w_grouped"), (3, "w_codes")):
             windows.setdefault(t, keep.tile([P, U], F32, name="window%d" % t, tag=tag, align_bytes=ALIGN))
@@ -122,12 +129,14 @@ def tile_picked_wroute2_linnone_lo_kernel(tc, x_words, x_scales, gate, w1, dst, 
 
         apply_gate(0, acc_0_first[:], 0, FIRST)
         scatter_on_scalar(0, 0, FIRST)
+        nc.scalar.copy(gated[1][:, HALF:], acc_1_high[:])
         apply_gate(0, acc_0_rest[:], FIRST, T)
         scatter_on_scalar(0, FIRST, T)
-        apply_gate(1, acc_1[:], 0, T)
+        apply_gate(1, acc_1_low[:], 0, HALF)
         apply_gate(2, acc_2[:], 0, T)
+        nc.vector.tensor_tensor(places(1, HALF, T), gated[1][:, HALF:], gate_sb[:, HALF:], MULT)
         apply_gate(3, acc_3[:], 0, T)
-        scatter_on_vector(1, 0, T)
+        scatter_on_vector(1, 0, HALF)
         scatter_on_scalar(2, 0, SHARED)
         nc.scalar.activation(places(3, 0, T), gated[3][:], COPY, scale=ones[:])
         scatter_on_vector(2, SHARED, T)
@@ -164,15 +173,16 @@ def tile_picked_wroute2_linnone_lo_kernel(tc, x_words, x_scales, gate, w1, dst, 
             nc.scalar.copy(grouped_words(U32, cols), paired_words(U32, cols))
 
         words_out = out_1[0].rearrange("p n t -> p (n t)").bitcast(I32)
-        for group in ((high, third), (second,), (first,)):
+        for group, queue in (((high, third), nc.scalar), ((second,), nc.scalar), ((first,), nc.sync)):
             for cols in group:
                 nc.vector.quantize_mx(
                     out=y_codes[:, cols].bitcast(FP8X4),
-                    scales=y_scales[:, cols],
+                    scales=y_scales[PACK * (cols.start // T) :, cols.start % T : cols.start % T + PIECE],
                     in_=y_grouped[:, PACK * cols.start : PACK * cols.stop],
                 )
             stored = slice(group[-1].start, group[0].stop)
-            nc.sync.dma_start(out=words_out[:, stored], in_=y_codes[:, stored].bitcast(I32))
-        for r in range(PACK):
-            queue = nc.sync if r % 2 else nc.scalar
-            queue.dma_start(out=out_2[0][r:BLOCKS:PACK, :].bitcast(I32), in_=y_scales[r:P:QUADRANT, :].bitcast(I32))
+            queue.dma_start(out=words_out[:, stored], in_=y_codes[:, stored].bitcast(I32))
+        scale_rows = out_2[0].bitcast(I32).rearrange("(q r) (a c) -> q a r c", r=PACK, a=2)
+        for q in range(PACK):
+            queue = nc.sync if q % 2 else nc.scalar
+            queue.dma_start(out=scale_rows[q], in_=y_scales[QUADRANT * q : QUADRANT * q + 2 * PACK, :].bitcast(I32))

@@ -26,6 +26,7 @@ SHARED = 192
 FIRST = 128
 SCALAR_M = 64
 LATE_M = 96
+EDGE = 64
 PIECE = 256
 ALIGN = 256
 
@@ -158,7 +159,7 @@ def tile_picked_wroute2_linnone_lo_kernel(tc, x_words, x_scales, gate, w1, dst, 
         for cols in halves[-2:]:
             nc.scalar.copy(out=pair_view[:, 1, cols, 1], in_=windows[3][:, cols])
         nc.vector.tensor_copy(out=pair_view[:, 1, : high.start, 0], in_=windows[2][:, : high.start])
-        for cols in (third, second, first):
+        for cols in (third, first, second):
             nc.vector.tensor_copy(out=pair_view[:, 1, cols, 1], in_=windows[3][:, cols])
 
         def grouped_words(dtype, cols):
@@ -167,13 +168,13 @@ def tile_picked_wroute2_linnone_lo_kernel(tc, x_words, x_scales, gate, w1, dst, 
         def paired_words(dtype, cols):
             return pairs[:].bitcast(dtype).rearrange("p (h c) -> p c h", h=2)[:, cols]
 
-        for cols in (third, halves[0]):
+        for cols in (third, slice(EDGE, first.stop)):
             nc.vector.tensor_copy(grouped_words(I32, cols), paired_words(I32, cols))
-        for cols in (halves[-2], halves[-1], second, halves[1]):
+        for cols in (halves[-2], halves[-1], slice(0, EDGE), second):
             nc.scalar.copy(grouped_words(U32, cols), paired_words(U32, cols))
 
         words_out = out_1[0].rearrange("p n t -> p (n t)").bitcast(I32)
-        for group, queue in (((high, third), nc.scalar), ((second,), nc.scalar), ((first,), nc.sync)):
+        for group, queue in (((high, third), nc.scalar), ((first,), nc.scalar), ((second,), nc.sync)):
             for cols in group:
                 nc.vector.quantize_mx(
                     out=y_codes[:, cols].bitcast(FP8X4),

from contextlib import ExitStack

import concourse.mybir as mybir

K, T, N, U = 512, 512, 512, 1024
FLOPS = 2 * K * T * N

F32 = mybir.dt.float32
BF16 = mybir.dt.bfloat16
I32 = mybir.dt.int32
U32 = mybir.dt.uint32
U16 = mybir.dt.uint16
U8 = mybir.dt.uint8
FP8X4 = mybir.dt.float8_e4m3fn_x4
MULT = mybir.AluOpType.mult
ADD = mybir.AluOpType.add
COPY = mybir.ActivationFunctionType.Copy

P = 128
PACK = 4
QUADRANT = 32
BLOCKS = 16
PER_COLUMN = 16
HALF = T // 2
SHARED = 192
FIRST = 128
SCALAR_M = 64
LATE_M = 96
EDGE = 64
PIECE = 256
ALIGN = 256


def tile_picked_wroute2_linnone_lo_kernel(tc, x_words, x_scales, gate, w1, dst, out_0, out_1, out_2):
    nc = tc.nc
    with ExitStack() as ctx:
        keep = ctx.enter_context(tc.tile_pool(name="keep", bufs=1))
        psum = ctx.enter_context(tc.psum_pool(name="psum", bufs=1))

        offsets = keep.tile([P, T // PER_COLUMN], U16, name="offsets")
        x_codes = keep.tile([P, T], U32, name="x_codes", align_bytes=ALIGN)
        x_plane = keep.tile([P, HALF], U8, name="x_plane", align_bytes=ALIGN)
        w_plane = keep.tile([P, N], U8, name="w_plane", align_bytes=ALIGN)
        gate_sb = keep.tile([P, T], F32, name="gate_sb", align_bytes=ALIGN)
        ones = keep.tile([P, 1], F32, name="ones")
        w_grouped = keep.tile([P, N * PACK], BF16, name="w_grouped", align_bytes=ALIGN)
        w_codes = keep.tile([P, N], U32, name="w_codes", align_bytes=ALIGN)
        y_codes = keep.tile([P, U], U32, name="y_codes", align_bytes=ALIGN)
        y_scales = keep.tile([P, U // 2], U8, name="y_scales", align_bytes=ALIGN)
        windows = {t: keep.tile([P, U], F32, name="window%d" % t, align_bytes=ALIGN) for t in (0, 1)}
        pairs = keep.tile([P, U * PACK], BF16, name="pairs", align_bytes=ALIGN)
        y_grouped = keep.tile([P, U * PACK], BF16, name="y_grouped", align_bytes=ALIGN)
        gated = [keep.tile([P, T], F32, name="gated%d" % t, align_bytes=ALIGN) for t in range(PACK)]
        w_raw = [keep.tile([P, 2, N], F32, name="w_raw%d" % u, align_bytes=ALIGN) for u in range(2)]

        w_rows = w1.rearrange("(p j) c -> p j c", j=PACK)
        x_rows = x_words[0].rearrange("p n t -> p (n t)").bitcast(I32)
        nc.sync.dma_start(out=w_raw[0][:], in_=w_rows[:, 0:2, :])
        x_scale_rows = x_scales[0].bitcast(I32).rearrange("(q r) (a c) -> q a r c", r=PACK, a=2)
        for q in range(PACK):
            nc.sync.dma_start(out=x_plane[QUADRANT * q : QUADRANT * q + 2 * PACK, :].bitcast(I32), in_=x_scale_rows[q])
        nc.sync.dma_start(out=w_raw[1][:], in_=w_rows[:, 2:4, :])
        nc.sync.dma_start(out=x_codes[:, :HALF].bitcast(I32), in_=x_rows[:, :HALF])
        nc.sync.dma_start(out=gate_sb[:, :HALF], in_=gate[:, :HALF])
        nc.sync.dma_start(offsets[:], dst)
        nc.sync.dma_start(out=x_codes[:, HALF:].bitcast(I32), in_=x_rows[:, HALF:])
        nc.sync.dma_start(out=gate_sb[:, HALF:], in_=gate[:, HALF:])

        for t in (0, 1):
            nc.vector.memset(windows[t][:].bitcast(I32), 0)
        nc.vector.memset(ones[:], 1.0)

        w_view = w_grouped[:].rearrange("p (t m j) -> p m t j", t=PACK, j=PACK)
        rows_01, rows_23 = (raw[:].rearrange("p j (m t) -> p m t j", t=PACK) for raw in w_raw)
        nc.scalar.copy(out=w_view[:, :SCALAR_M, :, 0:2], in_=rows_01[:, :SCALAR_M])
        nc.vector.tensor_copy(out=w_view[:, SCALAR_M:, :, 0:2], in_=rows_01[:, SCALAR_M:])
        nc.vector.tensor_copy(out=w_view[:, :LATE_M, 0, 2:4], in_=rows_23[:, :LATE_M, 0])
        nc.scalar.copy(out=w_view[:, LATE_M:, 0, 2:4], in_=rows_23[:, LATE_M:, 0])
        nc.scalar.copy(out=w_view[:, :LATE_M, 2:4, 2:4], in_=rows_23[:, :LATE_M, 2:4])
        nc.vector.tensor_copy(out=w_view[:, :, 1, 2:4], in_=rows_23[:, :, 1])

        def quantize_w(t0, t1):
            nc.vector.quantize_mx(
                out=w_codes[:, P * t0 : P * t1].bitcast(FP8X4),
                scales=w_plane[:, P * t0 : P * t1],
                in_=w_grouped[:, PACK * P * t0 : PACK * P * t1],
            )

        def project(t, *spans):
            base = min(a for a, b in spans)
            acc = psum.tile([P, max(b for a, b in spans) - base], F32, name="acc%d_%d" % (t, base))
            for a, b in spans:
                nc.tensor.matmul_mx(
                    out=acc[:, a - base : b - base],
                    lhsT=w_codes[:, P * t : P * (t + 1)].bitcast(FP8X4),
                    lhsT_scale=w_plane[:, P * t : P * (t + 1)],
                    rhs=x_codes[:, a:b].bitcast(FP8X4),
                    rhs_scale=x_plane[PACK * (a // HALF) :, a % HALF : a % HALF + b - a],
                    start=True,
                    stop=True,
                )
            return acc

        def apply_gate(t, acc, a, b):
            nc.vector.tensor_tensor(gated[t][:, a:b], acc, gate_sb[:, a:b], MULT)

        def places(t, a, b):
            return windows[t][:].indirect(offsets[:, a // PER_COLUMN : b // PER_COLUMN])

        def scatter_on_vector(t, a, b):
            nc.vector.tensor_copy(places(t, a, b), gated[t][:, a:b])

        def scatter_on_scalar(t, a, b):
            nc.scalar.activation(places(t, a, b), gated[t][:, a:b], COPY)

        quantize_w(0, 1)
        acc_0_first = project(0, (0, FIRST))
        quantize_w(1, 2)
        nc.vector.tensor_copy(out=w_view[:, LATE_M:, 2:4, 2:4], in_=rows_23[:, LATE_M:, 2:4])
        quantize_w(2, PACK)
        acc_0_rest = project(0, (FIRST, HALF), (HALF, T))
        acc_1_high = project(1, (HALF, T))
        acc_1_low = project(1, (0, HALF))
        acc_2 = project(2, (HALF, T), (0, HALF))
        acc_3 = project(3, (HALF, T), (0, HALF))

        for t, tag in ((2, "w_grouped"), (3, "w_codes")):
            windows.setdefault(t, keep.tile([P, U], F32, name="window%d" % t, tag=tag, align_bytes=ALIGN))
            nc.gpsimd.memset(windows[t][:].bitcast(I32), 0)

        apply_gate(0, acc_0_first[:], 0, FIRST)
        scatter_on_scalar(0, 0, FIRST)
        nc.scalar.copy(gated[1][:, HALF:], acc_1_high[:])
        apply_gate(0, acc_0_rest[:], FIRST, T)
        scatter_on_scalar(0, FIRST, T)
        apply_gate(1, acc_1_low[:], 0, HALF)
        apply_gate(2, acc_2[:], 0, T)
        nc.vector.tensor_tensor(places(1, HALF, T), gated[1][:, HALF:], gate_sb[:, HALF:], MULT)
        apply_gate(3, acc_3[:], 0, T)
        scatter_on_vector(1, 0, HALF)
        scatter_on_scalar(2, 0, SHARED)
        nc.scalar.activation(places(3, 0, T), gated[3][:], COPY, scale=ones[:])
        scatter_on_vector(2, SHARED, T)

        pair_view = pairs[:].rearrange("p (h c e) -> p h c e", h=2, e=2)
        out_rows = out_0.rearrange("(p t) c -> p t c", t=PACK)

        def store_window(t):
            nc.sync.dma_start(out=out_rows[:, t, :], in_=windows[t][:])

        for t in range(2):
            store_window(t)
            nc.gpsimd.tensor_scalar(pair_view[:, 0, :, t], windows[t][:], 1.0, -0.0, MULT, ADD)
        store_window(2)
        store_window(3)
        first, second, third, high = (slice(a, a + PIECE) for a in range(0, U, PIECE))
        halves = [slice(a, a + PIECE // 2) for a in range(0, U, PIECE // 2)]
        nc.scalar.copy(out=pair_view[:, 1, high, 0], in_=windows[2][:, high])
        for cols in halves[-2:]:
            nc.scalar.copy(out=pair_view[:, 1, cols, 1], in_=windows[3][:, cols])
        nc.vector.tensor_copy(out=pair_view[:, 1, : high.start, 0], in_=windows[2][:, : high.start])
        for cols in (third, first, second):
            nc.vector.tensor_copy(out=pair_view[:, 1, cols, 1], in_=windows[3][:, cols])

        def grouped_words(dtype, cols):
            return y_grouped[:].bitcast(dtype).rearrange("p (c h) -> p c h", h=2)[:, cols]

        def paired_words(dtype, cols):
            return pairs[:].bitcast(dtype).rearrange("p (h c) -> p c h", h=2)[:, cols]

        for cols in (third, slice(EDGE, first.stop)):
            nc.vector.tensor_copy(grouped_words(I32, cols), paired_words(I32, cols))
        for cols in (halves[-2], halves[-1], slice(0, EDGE), second):
            nc.scalar.copy(grouped_words(U32, cols), paired_words(U32, cols))

        words_out = out_1[0].rearrange("p n t -> p (n t)").bitcast(I32)
        for group, queue in (((high, third), nc.scalar), ((first,), nc.scalar), ((second,), nc.sync)):
            for cols in group:
                nc.vector.quantize_mx(
                    out=y_codes[:, cols].bitcast(FP8X4),
                    scales=y_scales[PACK * (cols.start // T) :, cols.start % T : cols.start % T + PIECE],
                    in_=y_grouped[:, PACK * cols.start : PACK * cols.stop],
                )
            stored = slice(group[-1].start, group[0].stop)
            queue.dma_start(out=words_out[:, stored], in_=y_codes[:, stored].bitcast(I32))
        scale_rows = out_2[0].bitcast(I32).rearrange("(q r) (a c) -> q a r c", r=PACK, a=2)
        for q in range(PACK):
            queue = nc.sync if q % 2 else nc.scalar
            queue.dma_start(out=scale_rows[q], in_=y_scales[QUADRANT * q : QUADRANT * q + 2 * PACK, :].bitcast(I32))
